import numpy as np, ml_dtypes
CORES = [242,247,114,119]
N = 4
BF = ml_dtypes.bfloat16
def gentries(a):
    return np.ascontiguousarray(a.reshape(8, 16, -1).transpose(0, 2, 1)).reshape(8, -1)
def gtable(e):
    e = np.asarray(e); return np.ascontiguousarray(e.reshape(8, -1, 16).transpose(0, 2, 1)).reshape(128, -1).astype(np.int32)
V, S, A, B, T = 1024, 384, 2048, 4, 4
W = V + (N - 1) * S
def parts(rng):
    z = np.exp2(rng.integers(-1, 2, (N, 8, 16, 1))).astype(np.float32); x = {}
    x["h"] = rng.standard_normal((N, 8, 16, V), dtype=np.float32) * z
    x["y"] = rng.standard_normal((N, 8, 16, T), dtype=np.float32) * z
    x["t"] = (z * (0.5 + rng.random(z.shape))).astype(np.float32)
    x["w"] = np.clip(rng.standard_normal((N, 8, 16, A), dtype=np.float32), -2, 2)
    x["M"] = int(rng.integers(0, 60000)) + rng.integers(0, 8, (N, 8, V)); x["m"] = rng.integers(0, A, (N, 8, V))
    x["pd"] = rng.integers(0, W, (N, 8, B, V)); x["lb"] = rng.integers(0, A, (N, 8, B, V)); x["sn"] = rng.integers(0, V, (N, 8, N - 1, S))
    return x
def pack(x):
    def c(a, n):
        v = np.ascontiguousarray(np.reshape(a, (N, 128, n))).astype(np.float32)
        return np.where(np.abs(v) < 2.0 ** -20, np.float32(0), v).astype(np.float32)
    return {"h0": c(x["h"], V), "mt": np.ascontiguousarray(x["M"]).astype(np.int32), "mm": np.ascontiguousarray(x["m"]).astype(np.int32), "wv": c(x["w"], A).astype(BF), "obs": c(x["y"], T), "th": c(x["t"], 1),
            "pd": np.stack([gtable(a.reshape(8, -1)) for a in x["pd"]]), "lb": np.stack([gtable(a.reshape(8, -1)) for a in x["lb"]]), "sn": np.stack([gtable(a.reshape(8, -1)) for a in x["sn"]])}
def at_ends(rng, lo, hi, v, share):
    return np.where(rng.random(v.shape) < share, np.where(rng.random(v.shape) < 0.5, lo, hi), v)
def setup_inputs(rng):
    return pack(parts(rng))
def setup_inputs_spread(rng):
    x = parts(rng)
    x["h"] = rng.standard_normal((N, 8, 16, V), dtype=np.float32) * np.exp2(rng.integers(-3, 3, (N, 8, 1, V))) * (rng.random((N, 8, 1, V)) > 0.0625)
    x["w"] = x["w"] * np.exp2(rng.integers(-4, 1, (N, 8, 1, A))) * (rng.random((N, 8, 1, A)) > 0.0625)
    top = 4096 * int(rng.integers(1, 15)); kind = np.arange(V) & 3
    x["M"] = np.where(kind == 0, top - 1, np.where(kind == 1, top, top - 12 + np.exp2(5 * rng.random((N, 8, V))).astype(np.int64)))
    s, p = x["sn"], x["pd"]; turn = (rng.integers(0, 2, (N, 8, 1, V)) + np.arange(B)[:, None]) & 1
    x["sn"] = s - (s & 3) + (np.arange(S) & 3)
    x["pd"] = np.where(kind == 3, p, p - (p & 3) + np.where(kind == 2, turn, kind))
    return pack(x)
def setup_inputs_ends(rng):
    x = parts(rng)
    x["M"] = 65535 * rng.integers(0, 2, (N, 8, V)); x["M"][:, 5:] = 65535; x["M"][:, 0] = 0
    x["m"] = (A - 1) * rng.integers(0, 2, (N, 8, V)); x["lb"] = at_ends(rng, 0, A - 1, x["lb"], 0.75)
    x["sn"] = at_ends(rng, 0, V - 1, x["sn"], 0.75); x["pd"] = at_ends(rng, 0, W - 1, x["pd"], 0.75)
    x["pd"][:, 7] = at_ends(rng, 0, V - 1, rng.integers(0, V, (N, B, V)), 0.75)
    x["w"] = at_ends(rng, -2, 2, x["w"], 0.7)
    x["t"][:, 0, :15] = 1024; x["t"][:, 7, :15] = 0
    for g in (0, 7):
        x["w"][:, g, 15] = rng.choice(np.array([0, 0, -2, 2]), (N, A)); x["h"][:, g, 15] = rng.choice(np.array([0, 1, -1]), (N, V))
        x["y"][:, g, 15] = 0; x["t"][:, g, 15] = 0
    few = [0, 1, V - 1]
    for g in (0, 7):
        x["pd"][:, g][..., few] = V - 1; x["m"][:, g][..., few] = A - 1
    x["lb"][:, 7][..., few] = A - 1; x["h"][:, 7, 15][..., few] = 1; x["h"][:, 0, 15][..., few] = 0
    a = A - 1
    for _ in range(T):
        a = (4 * a + A - 1) & (A - 1); x["w"][:, 7, 15, a] = 2
    return pack(x)
def setup_inputs_corners(rng):
    x = parts(rng)
    x["sn"][0::2, 1::2] = rng.choice(np.array([0, V - 1]), x["sn"][0::2, 1::2].shape); x["sn"][1::2, 0::2, N - 2] = V - 1
    for q in range(N):
        for g in range(8):
            p, l, kind = x["pd"][q, g], x["lb"][q, g], (g + q) & 7
            if kind == 0: p[:] = np.arange(V); x["M"][q, g] = 65535; x["m"][q, g] = A - 1
            if kind == 1: p[:] = 0; x["M"][q, g] = 0; x["m"][q, g] = 0
            if kind == 2: p[:] = W - 1
            if kind == 3: p[:] = V; p[B - 1, V - 1] = V - 1; x["M"][q, g, V - 1] = 0
            if kind == 4: p[1:] = p[0]; l[1:] = l[0]
            if kind == 5: p[1:] = p[0]; x["m"][q, g] = (A - 1) * rng.integers(0, 2, V)
            if kind == 6: x["t"][q, g] = 1024; x["M"][q, g] = 7
            if kind == 7: x["t"][q, g] = -1024 * (np.arange(16)[:, None] & 1); x["M"][q, g] = 65534 + rng.integers(0, 2, V); x["w"][q, g] = at_ends(rng, -2, 2, x["w"][q, g], 0.5)
    return pack(x)
def setup_inputs_calm(rng):
    x = parts(rng); u = (np.arange(8)[None, :] + np.arange(N)[:, None]) & 3
    x["M"] = u[:, :, None] + rng.integers(0, 2, (N, 8, V))
    n = (rng.random((N, 8, 1, A)) * (2 + u[:, :, None, None])).astype(np.int64)
    x["w"] = np.where(rng.random((N, 8, 16, A)) < 0.0625 * n, x["w"] * 2.0 ** -7, 2.0 ** -20 * rng.integers(-1, 2, (N, 8, 16, A)))
    x["h"] = x["h"] * np.float32(2.0 ** -10); x["t"] = (1 + rng.random((N, 8, 16, 1))).astype(np.float32)
    x["y"] = x["t"] * rng.choice(np.array([-1, 1]), (N, 8, 16, T))
    return pack(x)
def check_inputs(d):
    bad = []
    for k, lo, hi in (("mt", 0, 65535), ("mm", 0, A - 1), ("pd", 0, W - 1), ("lb", 0, A - 1), ("sn", 0, V - 1)):
        if np.min(d[k]) < lo or np.max(d[k]) > hi: bad.append("range of " + k)
    for k, hi in (("wv", 2), ("h0", 65536), ("obs", 65536), ("th", 65536)):
        v = np.abs(d[k].astype(np.float32))
        if not np.max(v) <= hi: bad.append("range of " + k)
        if not np.all((v == 0) | (v >= 2.0 ** -20)): bad.append("least size of " + k)
    return bad
def reference(h0, mt, mm, wv, obs, th, pd, lb, sn):
    h = h0.astype(np.float32).reshape(N, 8, 16, V); M = mt.astype(np.int64); m = mm.astype(np.int64)
    w = wv.astype(np.float32).reshape(N, 8, 16, A); y = obs.astype(np.float32).reshape(N, 8, 16, T); lim = th.astype(np.float32).reshape(N, 8, 16, 1)
    pl = np.stack([gentries(a) for a in pd]).astype(np.int64); ll = np.stack([gentries(a) for a in lb]).astype(np.int64)
    sl = np.stack([gentries(a) for a in sn]).astype(np.int64).reshape(N, 8, N - 1, S)
    for t in range(T):
        hw, Mw, mw = [h], [M], [m]
        for d in range(1, N):
            ix = sl[:, :, d - 1]
            hw.append(np.roll(np.take_along_axis(h, ix[:, :, None, :], 3), (d, -1), (0, 1)))
            Mw.append(np.roll(np.take_along_axis(M, ix, 2), (d, -1), (0, 1))); mw.append(np.roll(np.take_along_axis(m, ix, 2), (d, -1), (0, 1)))
        hp = np.take_along_axis(np.concatenate(hw, axis=3), pl[:, :, None, :], 3)
        Mp = np.take_along_axis(np.concatenate(Mw, axis=2), pl, 2); mp = np.take_along_axis(np.concatenate(mw, axis=2), pl, 2)
        a = (4 * mp + ll) & (A - 1)
        wa = np.take_along_axis(w, a[:, :, None, :], 3)
        e = y[..., t:t + 1] - hp * wa
        c = np.add.reduce((np.abs(e) > lim).astype(np.int64), axis=2)
        new = (Mp + c).reshape(N, 8, B, V); k = np.argmin(new, axis=2)
        pick = k * V + np.arange(V)
        M = np.min(new, axis=2); m = np.take_along_axis(a, pick, 2); p4 = pick[:, :, None, :]
        u = np.take_along_axis(e, p4, 3) * np.take_along_axis(wa, p4, 3)
        h = np.take_along_axis(hp, p4, 3) + np.float32(0.125) * u
    return {"yh": h.reshape(N, 128, V).astype(np.float32), "ymt": M.astype(np.float32), "ymm": m.astype(np.float32)}

@@ -1,0 +1,496 @@
+from concourse.bass import DstId, RemoteDMATransfer
+from concourse.mybir import AluOpType, ActivationFunctionType
+
+NV, NS, NA, NW, NT, NR = 1024, 384, 2048, 2176, 4, 4
+F, B, I, U16 = "float32", "bfloat16", "int32", "uint16"
+SCRATCH = {
+    "HW0": ("sbuf", [128, NW], F), "HW1": ("sbuf", [128, NW], F),
+    "AX0": ("sbuf", [128, NW], B), "AX1": ("sbuf", [128, NW], B),
+    "W2": ("sbuf", [128, 4096], B), "AG": ("sbuf", [128, 4096], B), "WA": ("sbuf", [128, 4096], B),
+    "PR": ("sbuf", [128, 4096], F), "RR": ("sbuf", [128, 4096], F), "FL": ("sbuf", [128, 4096], B),
+    "HR": ("sbuf", [128, NV], F), "SW": ("sbuf", [128, NV], B),
+    "SH": ("sbuf", [128, 1152], F), "SA": ("sbuf", [128, 1152], B),
+    "ES": ("sbuf", [128, NV], F), "UU": ("sbuf", [128, NV], F),
+    "UM": ("sbuf", [128, 16, 132], B),
+    "WC": ("sbuf", [128, 144], B), "WM": ("sbuf", [128, 144], B), "WL": ("sbuf", [128, 144], B),
+    "IB": ("sbuf", [128, 128], B), "I14": ("sbuf", [128, 128], B), "ZB": ("sbuf", [128, 128], B),
+    "IF": ("sbuf", [128, 128], F), "PF": ("sbuf", [128, 128], F),
+    "YI": ("sbuf", [128, 144], F), "T3": ("sbuf", [128, 16, 8], F),
+    "PI": ("sbuf", [128, 4], I), "PJ": ("sbuf", [128, 4], I), "CF": ("sbuf", [128, 16], F),
+    "CI": ("sbuf", [128, 64], I), "VI": ("sbuf", [128, 64], I),
+    "LP": ("sbuf", [128, 328], I), "LB": ("sbuf", [128, 256], I),
+    "ON": ("sbuf", [128, 328], U16), "OP": ("sbuf", [128, 328], U16),
+    "X1": ("sbuf", [128, 328], I), "X2": ("sbuf", [128, 328], F), "X3": ("sbuf", [128, 328], F), "X4": ("sbuf", [128, 328], I),
+    "MI": ("sbuf", [128, 128], I), "OB": ("sbuf", [128, 4], F), "O8": ("sbuf", [128, 4], F),
+    "TH": ("sbuf", [128, 4], F), "NTH": ("sbuf", [128, 4], F),
+    "ST": ("sbuf", [128, 4, 128], F), "SHI": ("sbuf", [128, 4, 128], B), "SLO": ("sbuf", [128, 4, 128], B),
+    "OA": ("sbuf", [128, 256], U16), "MN": ("sbuf", [128, 64], F), "MF": ("sbuf", [128, 64], F), "M2": ("sbuf", [128, 128], F), "RL": ("sbuf", [128, 256], B),
+    "PC": ("sbuf", [128, 256], B), "BE": ("sbuf", [128, 128], F), "KI": ("sbuf", [128, 128], I),
+    "TI": ("sbuf", [128, 128], I), "OI": ("sbuf", [128, 192], I), "OS": ("sbuf", [128, 192], U16),
+    "FO": ("sbuf", [128, 128], F), "FT": ("sbuf", [128, 128], F),
+    "K0": ("psum", [128, 512], F), "K1": ("psum", [128, 512], F), "K2": ("psum", [128, 512], F), "K3": ("psum", [128, 512], F),
+    "N0": ("psum", [128, 512], F), "N1": ("psum", [128, 512], F), "R0": ("psum", [128, 512], F), "R1": ("psum", [128, 512], F),
+}
+SEMAPHORES = (["cV", "cS", "cP", "cG", "locA", "locH", "dM", "dSN", "dHR", "dL", "dW", "dH", "dO", "dT", "dOwn", "dOut", "dOut2"]
+              + ["arrA%d" % t for t in range(NT)] + ["arrH%d" % t for t in range(NT)])
+
+ORDER = {
+    "V": "x0 x2 c0 x4 c1 x6 c2 o0 c3 w1 w4 m1 m2 p0 r0 r1 p1 r2 r3 p2 l1 p3 p4 g1 p5 p6 g3 p7 g5 b1 g6 g7 b2",
+    "S": "x1 x3 x5 x7 w0 w2 w3 m0 w5 w6 w7 a0 l0 g0 a1 a2 a3 g2 a4 a5 b0 g4 a6 a7",
+    "P": "A0 A1 M0 A2 A3 M1 M2 M3 K0 K1 K2 K3 E0 E1 E2 E3 Z0 C0 Z1 C1 C2 C3",
+}
+CH_STEP = (0, 20, 40, 54, 64)
+CH_LAST = (0, 12, 30, 50, 64)
+
+
+def rank_program(g, core, T, topo):
+    rank = T.rank_of(core)
+    if rank is None:
+        return
+    A, AF = AluOpType, ActivationFunctionType
+    Q = {"V": g.vector, "S": g.scalar, "P": g.tensor, "G": g, "Y": g.sync}
+    cnt, waited, lastw, readers, banks = {}, {}, {}, {}, {}
+
+    def wait(e, toks):
+        need = {}
+        for s, c in toks:
+            if e == "P" and s == "cP":
+                continue
+            need[s] = max(need.get(s, 0), c)
+        for s, c in need.items():
+            if waited.get((e, s), 0) < c:
+                Q[e].wait_ge(T.sem[s], c)
+                waited[(e, s)] = c
+
+    def deps(e, r, w, bk):
+        toks = [lastw[k] for k in r if k in lastw]
+        for k in w:
+            if k in lastw:
+                toks.append(lastw[k])
+            toks += readers.get(k, [])
+        for b in bk:
+            toks += [t for o, t in banks.get(b, {}).items() if o != e]
+        return toks
+
+    def done(e, tok, r, w, bk):
+        for k in r:
+            readers.setdefault(k, []).append(tok)
+        for k in w:
+            lastw[k] = tok
+            readers[k] = []
+        for b in bk:
+            banks.setdefault(b, {})[e] = tok
+
+    def op(e, fns, r=(), w=(), bk=()):
+        if not isinstance(fns, list):
+            fns = [fns]
+        wait(e, deps(e, r, w, bk))
+        s = "c" + e
+        for f in fns:
+            f().then_inc(T.sem[s], 1)
+            cnt[s] = cnt.get(s, 0) + 1
+        done(e, (s, cnt[s]), r, w, bk)
+
+    def dma(e, s, pairs, r=(), w=(), slow=False):
+        wait(e, deps(e, r, w, ()))
+        for o, i in pairs:
+            ins = Q[e].dma_start(o, i, allow_slow_non_contiguous=True) if slow else Q[e].dma_start(o, i)
+            ins.then_inc(T.sem[s], 16)
+            cnt[s] = cnt.get(s, 0) + 16
+        done(e, (s, cnt[s]), r, w, ())
+
+    def ts(out, in0, s1, o0, s2=None, o1=None):
+        if o1 is None:
+            return lambda: g.vector.tensor_scalar(out, in0, s1, None, o0)
+        return lambda: g.vector.tensor_scalar(out, in0, s1, s2, o0, o1)
+
+    def tt(out, a, b, o):
+        return lambda: g.vector.tensor_tensor(out, a, b, o)
+
+    def cp(out, a):
+        return lambda: g.vector.tensor_copy(out, a)
+
+    def act(out, a, f, **kw):
+        return lambda: g.scalar.activation(out, a, f, **kw)
+
+    def copy(e, out, a):
+        return cp(out, a) if e == "V" else act(out, a, AF.Copy)
+
+    def mm(out, l, rr, st, sp):
+        return lambda: g.tensor.matmul(out, l, rr, st, sp)
+
+    peers = {d: T.cores[(rank + d) % NR] for d in range(1, NR)}
+    near = [d for d in peers if peers[d] in topo.cores_of(core)]
+    far = [d for d in peers if d not in near]
+    far_eng = topo.engines(core, peers[far[0]])
+    eng = {}
+    for n, d in enumerate(far):
+        per = len(far_eng) // len(far)
+        eng[d] = far_eng[n * per:(n + 1) * per]
+    for d in near:
+        eng[d] = [x for x in topo.engines(core, peers[d]) if x not in far_eng]
+    arrive = sum(len(v) for v in eng.values())
+
+    def send(src, dst, ds, rsem, lsem, keys):
+        wait("G", deps("G", keys, (), ()))
+        trs = []
+        for d in ds:
+            rid, pid = topo.addr(peers[d], core)
+            trs.append(RemoteDMATransfer(dst_ids=[DstId(rid=rid, pnc=pid)], dma_engine_mask=sum(1 << x for x in eng[d]),
+                                         remote_sem=T.sem[rsem], src=src[:, (d - 1) * NS:d * NS],
+                                         dst=dst[:, NV + (d - 1) * NS:NV + d * NS]))
+            cnt[lsem] = cnt.get(lsem, 0) + len(eng[d])
+        g.remote_dma_fused(trs, local_sem=T.sem[lsem])
+
+    HW, AX = [T.HW0, T.HW1], [T.AX0, T.AX1]
+    K, N, R = [T.K0, T.K1, T.K2, T.K3], [T.N0, T.N1], [T.R0, T.R1]
+    CF = T.CF
+    c_p, c_pm, c_r, c_r7, c_g, c_show, c_mM, c_mL = [CF[:, j:j + 1] for j in range(8)]
+
+    dma("Y", "dM", [(T.MI[:, 0:64], T.mt[:]), (T.MI[:, 64:128], T.mm[:])], w=["MI"])
+    dma("S", "dSN", [(T.LP[0:112, 256:328], T.sn[16:128, :]), (T.LP[112:128, 256:328], T.sn[0:16, :])], w=["SN"])
+    dma("Y", "dHR", [(T.HR[0:112, :], T.h0[16:128, :]), (T.HR[112:128, :], T.h0[0:16, :])], w=["HR0", "HR1", "HR2", "HR3"])
+    dma("Y", "dL", [(T.LP[:, 0:256], T.pd[:]), (T.LB[:], T.lb[:]), (T.OB[:], T.obs[:])], w=["PD", "LB", "OB"])
+    dma("Y", "dW", [(T.W2[:, 0:NA], T.wv[:])], w=["W1"])
+    op("G", lambda: g.iota(T.PI[:], [[112, 4]], 0, 1), w=["PI"])
+    op("G", lambda: g.iota(T.T3[:], [[1, 16], [16, 8]], 0, 0, allow_small_or_imprecise_dtypes=True), w=["T3"])
+    op("G", lambda: g.iota(T.YI[:], [[1, 144]], 0, 0, allow_small_or_imprecise_dtypes=True), w=["YI"])
+    op("G", lambda: g.iota(T.CI[:], [[16, 64]], 0, 0), w=["CI"])
+    dma("G", "dT", [(T.TH[:, 0:1], T.th[:])], w=["TH"], slow=True)
+    op("V", lambda: g.vector.memset(T.UM[:], 0.0), w=["UM"])
+    op("V", ts(T.PJ[:, 0:2], T.PI[:, 0:2], 127, A.bitwise_and), r=["PI"], w=["PJa"])
+    op("V", ts(T.PJ[:, 2:3], T.PI[:, 0:1], 15, A.bitwise_and), r=["PI"], w=["PJb"])
+    op("V", ts(T.PJ[:, 3:4], T.PI[:, 0:1], 7, A.bitwise_and), r=["PI"], w=["PJc"])
+    op("V", cp(CF[:, 0:4], T.PJ[:]), r=["PJa", "PJb", "PJc"], w=["CF"])
+    op("V", [ts(T.UM[:, :, 3:131:16], T.T3[:], c_p, A.is_equal),
+             ts(T.UM[:, :, 11:131:16], T.T3[:], c_pm, A.is_equal)], r=["T3", "CF"], w=["UM"])
+    op("V", ts(c_show, c_r, 8.0, A.is_ge), r=["CF"], w=["c_show"])
+    op("V", ts(c_g, c_p, c_r, A.subtract, 15.0, A.add), r=["CF"], w=["c_g"])
+    op("V", ts(c_mM, c_r7, 3.0, A.is_lt), r=["CF"], w=["c_mM"])
+    op("V", ts(c_mL, c_r7, 3.0, A.is_equal, 4.0, A.mult), r=["CF"], w=["c_mL"])
+    op("V", ts(T.IB[:], T.YI[:, 0:128], c_p, A.is_equal), r=["YI", "CF"], w=["IB"])
+
+    def U(i, row):
+        return T.UM[:, i, 3 - row:131 - row]
+
+    pcs = [T.PC[:, 64 * j:64 * j + 64] for j in range(4)]
+    op("V", cp(pcs[0], T.MI[:, 0:64]), r=["MI"], w=["PC0"])
+    op("V", ts(T.TI[:, 0:64], T.MI[:, 64:128], 511, A.bitwise_and), r=["MI"], w=["TIa"])
+    op("V", tt(pcs[1], T.MI[:, 0:64], pcs[0], A.subtract), r=["MI", "PC0"], w=["PC1"])
+    op("V", ts(pcs[3], T.TI[:, 0:64], -256.0, A.add), r=["TIa"], w=["PC3"])
+    op("V", cp(T.ON[:, 256:328], T.LP[:, 256:328]), r=["SN"], w=["ONs"])
+    for b in range(2):
+        fns = []
+        for i in range(8 * b, 8 * b + 8):
+            o = N[b][:, 64 * (i % 8):64 * (i % 8) + 64]
+            fns += [mm(o, U(i, 0), pcs[0], True, False), mm(o, U(i, 1), pcs[1], False, False), mm(o, U(i, 3), pcs[3], False, True)]
+        op("P", fns, r=["UM", "PC0", "PC1", "PC3"], w=["N%d" % b], bk=["N%d" % b])
+    op("V", lambda: g.vector.memset(T.AX0[:, 0:NV], 0.0), w=["AX0o"])
+    op("V", ts(T.WL[:], T.YI[:], c_g, A.is_equal, c_mL, A.mult), r=["YI", "c_g", "c_mL"], w=["WL"])
+    op("V", ts(T.WM[:], T.YI[:], c_g, A.is_equal, c_mM, A.mult), r=["YI", "c_g", "c_mM"], w=["WM"])
+    op("V", ts(T.WC[:], T.YI[:], c_g, A.is_equal, 16384.0, A.mult), r=["YI", "c_g"], w=["WC"])
+    op("V", ts(T.PF[:], T.YI[:, 0:128], c_pm, A.is_equal), r=["YI", "CF"], w=["PF"])
+
+    hr_keys = ["HR0", "HR1", "HR2", "HR3"]
+
+    def show_h(e, c0, c1, key):
+        src = T.HR[:, 0:NV].indirect(T.ON[:, 256 + c0:256 + c1])
+        o = T.SH[:, 16 * c0:16 * c1]
+        op(e, cp(o, src) if e == "V" else act(o, src, AF.Copy), r=hr_keys + ["ONs"], w=[key])
+
+    def send_h(t):
+        send(T.SH, HW[t % 2], far, "arrH%d" % t, "locH", ["SH%d" % d for d in far])
+        if near:
+            send(T.SH, HW[t % 2], near, "arrH%d" % t, "locH", ["SH%d" % near[0], "SHx"])
+        for k in ["SH1", "SH2", "SH3", "SHx"]:
+            readers.setdefault(k, []).append(("locH", cnt["locH"]))
+        lastw["HW%dr" % (t % 2)] = ("arrH%d" % t, arrive)
+
+    def evac(b):
+        o = T.SW[:, 512 * b:512 * b + 512]
+        op("SV"[b], copy("SV"[b], o, N[b][:]), r=["N%d" % b], w=["SW%d" % b], bk=["N%d" % b])
+
+    def show_a(t):
+        off, key = (T.ON, "ONs") if t == 0 else (T.OP, "OP")
+        p = t % 2
+        dma("Y", "dOwn", [(AX[p][j:128:16, 0:NV], T.SW[j:128:16, :]) for j in range(4)], r=["SW0", "SW1"], w=["AX%do" % p])
+        op("V", ts(T.SA[:, 0:576], T.SW[:, 0:NV].indirect(off[:, 256:292]), c_show, A.mult), r=["SW0", "SW1", key, "c_show"], w=["SA0"])
+        op("S", act(T.SA[:, 576:1152], T.SW[:, 0:NV].indirect(off[:, 292:328]), AF.Identity, scale=c_show),
+           r=["SW0", "SW1", key, "c_show"], w=["SA1"])
+        send(T.SA, AX[p], far + near, "arrA%d" % t, "locA", ["SA0", "SA1"])
+        for k in ["SA0", "SA1"]:
+            readers.setdefault(k, []).append(("locA", cnt["locA"]))
+        lastw["AX%dr" % p] = ("arrA%d" % t, arrive)
+
+    evac(0)
+    evac(1)
+    show_a(0)
+    for d in far + near:
+        show_h("S", 24 * (d - 1), 24 * d, "SH%d" % d)
+    send_h(0)
+    dma("S", "dH", [(T.HW0[:, 0:NV], T.h0[:])], w=["HW0o0", "HW0o1", "HW0o2", "HW0o3"])
+
+    op("V", cp(T.ON[:, 0:256], T.LP[:, 0:256]), r=["PD"], w=["ONp"])
+    for k in range(4):
+        op("V", ts(T.ST[:, k, 0:64], T.LB[:, 64 * k:64 * k + 64], 1024.0 + 4096 * k, A.add), r=["LB"], w=["STa%d" % k])
+        op("V", ts(T.ST[:, k, 64:128], T.LP[:, 64 * k:64 * k + 64], 4096.0 * k, A.add), r=["PD"], w=["STb%d" % k])
+    stk = ["STa%d" % k for k in range(4)] + ["STb%d" % k for k in range(4)]
+    op("S", act(T.SHI[:, :, 0:128], T.ST[:], AF.Copy), r=stk, w=["SHI"])
+    op("V", ts(T.X4[:], T.LP[:], 1023.0, A.min), r=["PD", "SN"], w=["X4"])
+    op("V", ts(T.X3[:], T.LP[:], 1023.0, A.min, 0.9375, A.mult), r=["PD", "SN"], w=["X3"])
+    op("V", ts(T.X1[:], T.X4[:], 15, A.bitwise_and), r=["X4"], w=["X1"])
+    op("V", tt(T.SLO[:], T.ST[:], T.SHI[:, :, 0:128], A.subtract), r=stk + ["SHI"], w=["SLO"])
+    op("S", act(T.I14[:], T.IB[:], AF.Copy, scale=16384.0), r=["IB"], w=["I14"])
+    op("S", act(T.ZB[:], T.IB[:], AF.Copy, scale=0.0), r=["IB"], w=["ZB"])
+    op("S", act(T.O8[:], T.OB[:], AF.Copy, scale=0.125), r=["OB"], w=["O8"])
+    op("S", act(T.W2[:, NA:2 * NA], T.W2[:, 0:NA], AF.Copy), r=["W1"], w=["W2"])
+    op("S", act(T.NTH[:, 0:1], T.TH[:, 0:1], AF.Copy, scale=-1.0), r=["TH"], w=["NTH"])
+    op("S", act(T.IF[:], T.IB[:], AF.Copy), r=["IB"], w=["IF"])
+    op("S", act(T.AX1[:, 0:NV], T.W2[:, 0:NV], AF.Copy, scale=0.0), r=["W1"], w=["AX1o"])
+    op("V", ts(T.X2[:], T.X1[:], 63.9375, A.mult), r=["X1"], w=["X2"])
+    op("V", tt(T.X3[:], T.LP[:], T.X3[:], A.subtract), r=["PD", "SN"], w=["X3"])
+    op("V", ts(T.VI[:], T.CI[:], c_r, A.add), r=["CI", "CF"], w=["VI"])
+
+    def late_constants(j):
+        op("V", tt(T.X1[:], T.X2[:], T.X3[:], A.add), r=["X2", "X3"], w=["X1"])
+        op("V", cp(T.OP[:], T.X1[:]), r=["X1"], w=["OP"])
+
+    def wrap(out, w, src, k, last, first=False):
+        return [mm(out, w[:, 15 - i:143 - i], src[:, 1024 * k + i:1024 * k + 1024:16], first and i == 0, last and i == 15) for i in range(16)]
+
+    def ps_a(k):
+        return R[k % 2][:, 128 * (k // 2):128 * (k // 2) + 64]
+
+    def ps_m(k):
+        return N[k // 2][:, 64 * (k % 2):64 * (k % 2) + 64]
+
+    def ps_b(k):
+        return R[0][:, 256:320] if k == 3 else K[k][:, 64:128]
+
+    for t in range(NT):
+        p, q = t % 2, (t + 1) % 2
+        last = t == NT - 1
+        off, okey = (T.ON, "ONp") if t == 0 else (T.OP, "OP")
+        hwk = ["HW%do%d" % (p, j) for j in range(4)] + ["HW%dr" % p]
+        y, y8 = T.OB[:, t:t + 1], T.O8[:, t:t + 1]
+
+        def sl(buf, j):
+            return buf[:, 512 * j:512 * j + 512]
+
+        def aux(e, j):
+            src = AX[p][:, 0:NW].indirect(off[:, 32 * j:32 * j + 32])
+            op(e, copy(e, sl(T.AG, j), src),
+               r=["AX%do" % p, "AX%dr" % p, okey], w=["AG%d" % j])
+
+        def mwrap(k):
+            o = ps_a(k)
+            op("P", [mm(o, T.IB[:], T.SHI[:, k, 0:64], True, False), mm(o, T.IB[:], T.SLO[:, k, 0:64], False, False)]
+               + wrap(o, T.WL, T.AG, k, True),
+               r=["IB", "SHI", "SLO", "WL", "AG%d" % (2 * k), "AG%d" % (2 * k + 1)], w=["PA%d" % k], bk=["R%d" % (k % 2)])
+
+        def conv(k):
+            op("V", ts(T.OA[:, 64 * k:64 * k + 64], ps_a(k), -4096.0 * k, A.add), r=["PA%d" % k], w=["OA%d" % k], bk=["R%d" % (k % 2)])
+
+        def Mwrap(k):
+            op("P", wrap(ps_m(k), T.WM, T.AG, k, True, first=True), r=["WM", "AG%d" % (2 * k), "AG%d" % (2 * k + 1)],
+               w=["KM%d" % k], bk=["N%d" % (k // 2)])
+
+        def keys(k):
+            n = 64 if k == 3 else 128
+            o = K[k][:, 0:n]
+            op("P", [mm(o, T.IB[:], T.SHI[:, k, 0:n], True, False), mm(o, T.IB[:], T.SLO[:, k, 0:n], False, False)]
+               + wrap(K[k][:, 0:64], T.WL, T.AG, k, False),
+               r=["IB", "SHI", "SLO", "WL", "AG%d" % (2 * k), "AG%d" % (2 * k + 1)], w=["KA%d" % k, "KB%d" % k], bk=["K%d" % k])
+
+        def wa(e, j):
+            src = T.W2[:, 0:4096].indirect(T.OA[:, 32 * j:32 * j + 32])
+            op(e, copy(e, sl(T.WA, j), src), r=["W2", "OA%d" % (j // 2)], w=["WA%d" % j])
+
+        def least(e, j):
+            if j == 0:
+                op(e, copy(e, T.M2[:], N[0][:, 0:128]), r=["KM0", "KM1"], w=["M2"], bk=["N0"])
+            elif j == 1:
+                op("V", tt(T.M2[:], T.M2[:], N[1][:, 0:128], A.min), r=["KM2", "KM3"], w=["M2"], bk=["N1"])
+            else:
+                op("V", tt(T.MN[:], T.M2[:, 0:64], T.M2[:, 64:128], A.min), r=["M2"], w=["MN"])
+
+        def rel(e, k):
+            op("V", tt(T.RL[:, 64 * k:64 * k + 64], ps_m(k), T.MN[:], A.subtract), r=["KM%d" % k, "MN"], w=["RL%d" % k], bk=["N%d" % (k // 2)])
+
+        def addrel(e, k):
+            rl = T.RL[:, 64 * k:64 * k + 64]
+            fns = [mm(K[k][:, 0:64], T.I14[:], rl, False, False)]
+            if k == 3:
+                fns += [mm(ps_b(3), T.IB[:], T.SHI[:, 3, 64:128], True, False), mm(ps_b(3), T.IB[:], T.SLO[:, 3, 64:128], False, False)]
+            op("P", fns + [mm(ps_b(k), T.I14[:], rl, False, False)],
+               r=["I14", "RL%d" % k], w=["KA%d" % k, "KB%d" % k], bk=["K%d" % k] + (["R0"] if k == 3 else []))
+
+        def split(e, j):
+            if last:
+                if j == 1:
+                    op("V", ts(T.MF[:], T.MN[:], -192.0 * (NT - 1), A.add), r=["MN"], w=["MF"])
+            elif j == 0:
+                op(e, copy(e, pcs[0], T.MN[:]), r=["MN"], w=["PC0"])
+            else:
+                op("V", tt(pcs[1], T.MN[:], pcs[0], A.subtract), r=["MN", "PC0"], w=["PC1"])
+
+        def unwrap1(e, b):
+            if last:
+                return
+            fns = [mm(N[b][:], T.ZB[:], T.W2[:, 0:512], True, False)]
+            for i in range(8 * b, 8 * b + 8):
+                o = N[b][:, 64 * (i % 8):64 * (i % 8) + 64]
+                fns += [mm(o, U(i, 0), pcs[0], False, False), mm(o, U(i, 1), pcs[1], False, False)]
+            op("P", fns, r=["UM", "ZB", "W2", "PC0", "PC1"], w=["N%d" % b], bk=["N%d" % b])
+
+        def prod(j):
+            op("V", tt(sl(T.PR, j), HW[p][:, 0:NW].indirect(T.ON[:, 32 * j:32 * j + 32]), sl(T.WA, j), A.mult),
+               r=hwk + ["ONp", "WA%d" % j], w=["PR%d" % j])
+
+        def absd(j):
+            op("S", act(sl(T.RR, j), sl(T.PR, j), AF.Abs, bias=y, scale=-1.0), r=["PR%d" % j, "OB"], w=["RR%d" % j])
+
+        def gt(j):
+            op("V", ts(sl(T.FL, j), sl(T.RR, j), T.TH[:, 0:1], A.is_gt), r=["RR%d" % j, "TH"], w=["FL%d" % j])
+
+        def helpgt(j):
+            op("S", act(sl(T.FL, j), sl(T.RR, j), AF.Sign, bias=T.NTH[:, 0:1]), r=["RR%d" % j, "NTH"], w=["FL%d" % j])
+            op("S", act(sl(T.FL, j), sl(T.FL, j), AF.Relu), w=["FL%d" % j])
+
+        def count(k, which):
+            o = K[k][:, 0:64] if which == "A" else ps_b(k)
+            op("P", wrap(o, T.WC, T.FL, k, which == "B" or k == 3), r=["WC", "FL%d" % (2 * k), "FL%d" % (2 * k + 1)],
+               w=["K%s%d" % (which, k)], bk=["R0" if which == "B" and k == 3 else "K%d" % k])
+
+        def best(e, k):
+            src = K[k][:, 0:128]
+            op(e, copy(e, T.BE[:], src) if k == 0 else tt(T.BE[:], T.BE[:], src, A.min), r=["KA%d" % k, "KB%d" % k], w=["BE"], bk=["K%d" % k])
+
+        def counts(e, k):
+            count(k, "A")
+            count(k, "B")
+
+        def late(e, j):
+            if t == 0:
+                late_constants(j)
+
+        make = {"x": aux, "c": lambda e, k: conv(k), "w": wa, "m": least, "r": rel, "l": split, "b": best, "o": late,
+                "p": lambda e, j: prod(j), "a": lambda e, j: absd(j), "g": lambda e, j: gt(j) if e == "V" else helpgt(j),
+                "A": lambda e, k: mwrap(k), "M": lambda e, k: Mwrap(k), "K": lambda e, k: keys(k), "E": addrel, "Z": unwrap1, "C": counts}
+
+        def needs(x):
+            kind, j = x[0], int(x[1])
+            two = ["%s%d" % ({"A": "x", "M": "x", "K": "x", "C": "g"}.get(kind, ""), 2 * j + n) for n in range(2)]
+            return {"x": [], "o": [], "A": two, "M": two, "K": two, "c": ["A%d" % j], "w": ["c%d" % (j // 2)],
+                    "m": [["M0", "M1"], ["m0", "M2", "M3"], ["m1"]][min(j, 2)], "r": ["m2"], "l": ["m2"] if j == 0 else ["l0"],
+                    "E": ["r%d" % j, "K%d" % j] + (["c0", "c2"] if j == 3 else []), "Z": ["l1", "r0", "r1", "r2", "r3"],
+                    "p": ["w%d" % j], "a": ["p%d" % j], "g": ["a%d" % j], "C": two + ["E%d" % j],
+                    "b": ["C%d" % j] + (["b%d" % (j - 1)] if j else [])}[kind]
+
+        todo, made = {e: ORDER[e].split() for e in "VSP"}, set()
+        while any(todo.values()):
+            moved = False
+            for e in "VSP":
+                while todo[e] and all(n in made for n in needs(todo[e][0])):
+                    x = todo[e].pop(0)
+                    make[x[0]](e, int(x[1]))
+                    made.add(x)
+                    moved = True
+            if not moved:
+                raise ValueError("the orders of the queues don't fit")
+
+        KA, KB = T.KI[:, 0:64], T.KI[:, 64:128]
+        op("V", tt(KA, T.BE[:, 0:64], K[3][:, 0:64], A.min), r=["BE", "KA3"], w=["KIa"], bk=["K3"])
+        if not last:
+            op("V", ts(T.TI[:, 0:64], KA, 511, A.bitwise_and), r=["KIa"], w=["TIa"])
+            op("V", ts(pcs[2], KA, 2.0 ** -14, A.mult, 191.5 + 2.0 ** -15, A.add), r=["KIa"], w=["PC2"])
+            op("V", ts(pcs[3], T.TI[:, 0:64], -256.0, A.add), r=["TIa"], w=["PC3"])
+            for b in range(2):
+                fns = []
+                for i in range(8 * b, 8 * b + 8):
+                    o = N[b][:, 64 * (i % 8):64 * (i % 8) + 64]
+                    fns += [mm(o, U(i, 2), pcs[2], False, False), mm(o, U(i, 3), pcs[3], False, i % 8 == 7)]
+                op("P", fns, r=["UM", "PC2", "PC3"], w=["N%d" % b], bk=["N%d" % b])
+        op("V", ts(T.TI[:, 64:128], KA, 2, A.logical_shift_right, 3072, A.bitwise_and), r=["KIa"], w=["TIb"])
+        if last:
+            op("V", ts(T.MI[:, 0:64], KA, 14, A.logical_shift_right), r=["KIa"], w=["MI", "MIa"])
+            op("V", ts(T.MI[:, 64:128], KA, 2047, A.bitwise_and), r=["KIa"], w=["MIb"])
+        op("V", tt(KB, T.BE[:, 64:128], ps_b(3), A.min), r=["BE", "KB3"], w=["KIb"], bk=["R0"])
+        op("V", tt(T.OI[:, 128:192], T.TI[:, 64:128], T.VI[:], A.add), r=["TIb", "VI"], w=["OIb"])
+        op("V", ts(T.OI[:, 0:128], T.KI[:], 4095, A.bitwise_and), r=["KIa", "KIb"], w=["OIa"])
+        op("V", cp(T.OS[:], T.OI[:]), r=["OIa", "OIb"], w=["OS"])
+
+        prk = ["PR%d" % j for j in range(8)]
+        CH = CH_LAST if last else CH_STEP
+
+        def c4(buf, j):
+            return buf[:, 16 * CH[j]:16 * CH[j + 1]]
+
+        def o4(c0, j):
+            return T.OS[:, c0 + CH[j]:c0 + CH[j + 1]]
+
+        def es(j):
+            op("S", act(c4(T.ES, j), T.PR[:, 0:4096].indirect(o4(128, j)), AF.Identity, bias=y8, scale=-0.125),
+               r=prk + ["OS", "O8"], w=["ES%d" % j])
+
+        def uu(j):
+            op("V", tt(c4(T.UU, j), T.W2[:, 0:4096].indirect(o4(0, j)), c4(T.ES, j), A.mult), r=["W2", "OS", "ES%d" % j], w=["UU%d" % j])
+
+        def hn(j):
+            op("V", tt(c4(HW[q], j), HW[p][:, 0:NW].indirect(o4(64, j)), c4(T.UU, j), A.add),
+               r=hwk + ["OS", "UU%d" % j], w=["HW%do%d" % (q, j)])
+            if last:
+                dma("S", "dO", [(c4(T.yh, j), c4(HW[q], j))], r=["HW%do%d" % (q, j)])
+                return
+            op("P", mm(K[j][:, 0:16 * (CH[j + 1] - CH[j])], T.PF[:], c4(HW[q], j), True, True), r=["PF", "HW%do%d" % (q, j)], w=["R%d" % j], bk=["K%d" % j])
+
+        def rot(j):
+            op("S", act(c4(T.HR, j), K[j][:, 0:16 * (CH[j + 1] - CH[j])], AF.Copy), r=["R%d" % j], w=["HR%d" % j], bk=["K%d" % j])
+
+        if not last:
+            evac(0)
+            evac(1)
+            es(0)
+            show_a(t + 1)
+            es(1)
+            uu(0)
+            uu(1)
+            es(2)
+            hn(0)
+            es(3)
+            uu(2)
+            hn(1)
+            rot(0)
+            uu(3)
+            rot(1)
+            hn(2)
+            hn(3)
+            rot(2)
+            rot(3)
+            show_h("V", 24 * (far[0] - 1), 24 * far[0], "SH%d" % far[0])
+            show_h("S", 24 * (far[1] - 1), 24 * far[1], "SH%d" % far[1])
+            c0 = 24 * (near[0] - 1)
+            show_h("V", c0, c0 + 12, "SH%d" % near[0])
+            show_h("S", c0 + 12, c0 + 24, "SHx")
+            send_h(t + 1)
+        else:
+            es(0)
+            op("V", tt(T.FO[:, 0:64], T.MI[:, 0:64], T.MF[:], A.add), r=["MIa", "MF"], w=["FOa"])
+            op("V", cp(T.FO[:, 64:128], T.MI[:, 64:128]), r=["MIb"], w=["FOb"])
+            es(1)
+            uu(0)
+            op("P", lambda: g.tensor.transpose(N[0][:, 0:128], T.FO[:], T.IF[:]), r=["FOa", "FOb", "IF"], w=["N0"], bk=["N0"])
+            op("S", act(T.FT[:], N[0][:, 0:128], AF.Copy), r=["N0"], w=["FT"], bk=["N0"])
+            dma("Y", "dOut", [(T.ymt[gg, :], T.FT[0:64, 16 * gg:16 * gg + 16]) for gg in range(8)]
+                + [(T.ymm[gg, :], T.FT[64:128, 16 * gg:16 * gg + 16]) for gg in range(8)], r=["FT"])
+            es(2)
+            es(3)
+            uu(1)
+            hn(0)
+            uu(2)
+            hn(1)
+            uu(3)
+            hn(2)
+            hn(3)
+
+    wait("G", [(s, c) for s, c in cnt.items()])

@@ -1,46 +1,65 @@
 from concourse.bass import DstId, RemoteDMATransfer
 from concourse.mybir import AluOpType, ActivationFunctionType
 
-NV, NS, NA, NW, NT, NR = 1024, 384, 2048, 2176, 4, 4
+NV, NS, NA, NW, NT, NR, NC = 1024, 384, 2048, 2176, 4, 4, 256
 F, B, I, U16 = "float32", "bfloat16", "int32", "uint16"
 SCRATCH = {
     "HW0": ("sbuf", [128, NW], F), "HW1": ("sbuf", [128, NW], F),
-    "AX0": ("sbuf", [128, NW], B), "AX1": ("sbuf", [128, NW], B),
-    "W2": ("sbuf", [128, 4096], B), "AG": ("sbuf", [128, 4096], B), "WA": ("sbuf", [128, 4096], B),
+    "AX": ("sbuf", [128, NW], B), "AC0": ("sbuf", [128, NR * NC], B), "AC1": ("sbuf", [128, NR * NC], B),
+    "W0": ("sbuf", [128, 4096], B), "W1": ("sbuf", [128, 4096], B), "MK": ("sbuf", [128, 4096], B), "AG": ("sbuf", [128, 4096], B), "WA": ("sbuf", [128, 4096], B),
     "PR": ("sbuf", [128, 4096], F), "RR": ("sbuf", [128, 4096], F), "FL": ("sbuf", [128, 4096], B),
-    "HR": ("sbuf", [128, NV], F), "SW": ("sbuf", [128, NV], B),
+    "HR": ("sbuf", [128, NV], F), "SW": ("sbuf", [128, NV], B), "SX": ("sbuf", [128, NV], B), "SC": ("sbuf", [128, NC], B),
     "SH": ("sbuf", [128, 1152], F), "SA": ("sbuf", [128, 1152], B),
     "ES": ("sbuf", [128, NV], F), "UU": ("sbuf", [128, NV], F),
-    "UM": ("sbuf", [128, 16, 132], B),
-    "WC": ("sbuf", [128, 144], B), "WM": ("sbuf", [128, 144], B), "WL": ("sbuf", [128, 144], B),
-    "IB": ("sbuf", [128, 128], B), "I14": ("sbuf", [128, 128], B), "ZB": ("sbuf", [128, 128], B),
-    "IF": ("sbuf", [128, 128], F), "PF": ("sbuf", [128, 128], F),
-    "YI": ("sbuf", [128, 144], F), "T3": ("sbuf", [128, 16, 8], F),
-    "PI": ("sbuf", [128, 4], I), "PJ": ("sbuf", [128, 4], I), "CF": ("sbuf", [128, 16], F),
+    "UM": ("sbuf", [128, 16, 132], B), "CM": ("sbuf", [128, 4, 168], B),
+    "WC": ("sbuf", [128, 144], B), "WX": ("sbuf", [128, 144], B),
+    "WM0": ("sbuf", [128, 144], B), "WL0": ("sbuf", [128, 144], B), "WM1": ("sbuf", [128, 256], B), "WL1": ("sbuf", [128, 256], B),
+    "IW": ("sbuf", [128, 256], B), "I14": ("sbuf", [128, 128], B), "ZB": ("sbuf", [128, 128], B),
+    "IF": ("sbuf", [128, 128], F),
+    "YI": ("sbuf", [128, 256], F), "T3": ("sbuf", [128, 16, 8], F), "CC": ("sbuf", [128, NC], B),
+    "PI": ("sbuf", [128, 4], I), "PJ": ("sbuf", [128, 4], I), "CF": ("sbuf", [128, 24], F),
     "CI": ("sbuf", [128, 64], I), "VI": ("sbuf", [128, 64], I),
     "LP": ("sbuf", [128, 328], I), "LB": ("sbuf", [128, 256], I),
-    "ON": ("sbuf", [128, 328], U16), "OP": ("sbuf", [128, 328], U16),
-    "X1": ("sbuf", [128, 328], I), "X2": ("sbuf", [128, 328], F), "X3": ("sbuf", [128, 328], F), "X4": ("sbuf", [128, 328], I),
-    "MI": ("sbuf", [128, 128], I), "OB": ("sbuf", [128, 4], F), "O8": ("sbuf", [128, 4], F),
-    "TH": ("sbuf", [128, 4], F), "NTH": ("sbuf", [128, 4], F),
+    "ON": ("sbuf", [128, NT * 328], U16), "OC": ("sbuf", [128, 256], U16), "DD": ("sbuf", [128, 3, 256], B),
+    "MI": ("sbuf", [128, 128], I), "OB": ("sbuf", [128, 4], F), "TH": ("sbuf", [128, 4], F),
+    "CB": ("sbuf", [128, NT * 16], F),
     "ST": ("sbuf", [128, 4, 128], F), "SHI": ("sbuf", [128, 4, 128], B), "SLO": ("sbuf", [128, 4, 128], B),
-    "OA": ("sbuf", [128, 256], U16), "MN": ("sbuf", [128, 64], F), "MF": ("sbuf", [128, 64], F), "M2": ("sbuf", [128, 128], F), "RL": ("sbuf", [128, 256], B),
+    "OA": ("sbuf", [128, 256], U16), "MN": ("sbuf", [128, 64], F), "M2": ("sbuf", [128, 128], F), "RL": ("sbuf", [128, 256], B),
     "PC": ("sbuf", [128, 256], B), "BE": ("sbuf", [128, 128], F), "KI": ("sbuf", [128, 128], I),
-    "TI": ("sbuf", [128, 128], I), "OI": ("sbuf", [128, 192], I), "OS": ("sbuf", [128, 192], U16),
-    "FO": ("sbuf", [128, 128], F), "FT": ("sbuf", [128, 128], F),
+    "TI": ("sbuf", [128, 128], I), "OI": ("sbuf", [128, 128], I), "OS": ("sbuf", [128, 128], U16),
+    "FO": ("sbuf", [128, 128], F), "FT": ("sbuf", [32, 8, 4, 16], F),
     "K0": ("psum", [128, 512], F), "K1": ("psum", [128, 512], F), "K2": ("psum", [128, 512], F), "K3": ("psum", [128, 512], F),
     "N0": ("psum", [128, 512], F), "N1": ("psum", [128, 512], F), "R0": ("psum", [128, 512], F), "R1": ("psum", [128, 512], F),
 }
-SEMAPHORES = (["cV", "cS", "cP", "cG", "locA", "locH", "dM", "dSN", "dHR", "dL", "dW", "dH", "dO", "dT", "dOwn", "dOut", "dOut2"]
-              + ["arrA%d" % t for t in range(NT)] + ["arrH%d" % t for t in range(NT)])
+SEMAPHORES = (["cV", "cS", "cP", "cG", "locA", "locH0", "locH1", "dM", "dSN", "dHR", "dL", "dH", "dO", "dT", "dR", "dOwn", "dOH", "dOut"]
+              + ["dW%d" % t for t in range(NT)] + ["arrA%d" % t for t in range(NT)] + ["arrH%d" % t for t in range(NT)])
 
-ORDER = {
-    "V": "x0 x2 c0 x4 c1 x6 c2 o0 c3 w1 w4 m1 m2 p0 r0 r1 p1 r2 r3 p2 l1 p3 p4 g1 p5 p6 g3 p7 g5 b1 g6 g7 b2",
-    "S": "x1 x3 x5 x7 w0 w2 w3 m0 w5 w6 w7 a0 l0 g0 a1 a2 a3 g2 a4 a5 b0 g4 a6 a7",
-    "P": "A0 A1 M0 A2 A3 M1 M2 M3 K0 K1 K2 K3 E0 E1 E2 E3 Z0 C0 Z1 C1 C2 C3",
+MAIN0 = {
+    "V": "x0 x2 c01 x4 w0 c23 x6 c45 w4 c67 m1 p0 m2 p1 r0 r1 r2 r3 p2 l1 p3 p4 g1 p5 g2 p6 g3 p7 o0 g5 b1 i6 i7 j7 b2",
+    "S": "x1 x3 x5 x7 w1 m0 w2 w3 w5 w6 w7 l0 a0 a1 a2 a3 g0 a4 a5 g4 b0 a6 a7 j6",
+    "P": "A01 A23 M0 M1 A45 A67 M2 M3 K0 K1 K2 K3 X0 E0 E1 E2 E3 Z0 C0 C1 C2 C3 C4",
+    "G": "L0",
 }
-CH_STEP = (0, 20, 40, 54, 64)
-CH_LAST = (0, 12, 30, 50, 64)
+MAIN = {
+    "V": "x0 x1 c0 x2 c1 x3 c2 x4 c3 x5 c4 x6 c5 x7 c6 p0 c7 p1 m1 m2 p2 r0 r1 r2 r3 p3 p4 l1 p5 g1 p6 g3 p7 g4 g5 b1 i6 i7 j7 b2",
+    "S": "w0 w1 w2 w3 w4 w5 m0 w6 a0 w7 a1 l0 g0 a2 a3 g2 a4 a5 b0 a6 a7 j6",
+    "P": "A0 A1 A2 A3 M0 A4 A5 M1 A6 A7 M2 M3 K0 K1 K2 K3 E0 E1 E2 E3 C0 C1 Z0 C2 C3 C4",
+    "G": "L0",
+}
+TAIL = {
+    "V": "n0 n1 n2 n4 n3 n5 n6 v0 u0 b3 n7 n8 u1 n9 h0 h1 u2 u3 h2 h3 s0",
+    "S": "e0 e1 e2 e3 s1 s2 s3",
+    "P": "C5 Y0 C6",
+    "G": "t0 t1 t2 k03",
+}
+LAST = {
+    "V": "n0 n4 n2 n5 n1 n6 f0 b3 n7 u0 n8 n9 h0 u1 h1 u2 h2 u3 h3",
+    "S": "e0 e1 e2 e3 f2",
+    "P": "C5 C6 f1",
+    "G": "k0 k1 k2 k3",
+}
+CH_STEP = (0, 8, 28, 50, 64)
+CH_LAST = (0, 12, 32, 54, 64)
 
 
 def rank_program(g, core, T, topo):
@@ -131,180 +150,216 @@ def rank_program(g, core, T, topo):
         eng[d] = [x for x in topo.engines(core, peers[d]) if x not in far_eng]
     arrive = sum(len(v) for v in eng.values())
 
-    def send(src, dst, ds, rsem, lsem, keys):
+    alone = {d: topo.engines(core, peers[d]) for d in near}
+
+    def send(src, dst, ds, rsem, lsem, keys, eng=eng):
         wait("G", deps("G", keys, (), ()))
         trs = []
         for d in ds:
             rid, pid = topo.addr(peers[d], core)
             trs.append(RemoteDMATransfer(dst_ids=[DstId(rid=rid, pnc=pid)], dma_engine_mask=sum(1 << x for x in eng[d]),
-                                         remote_sem=T.sem[rsem], src=src[:, (d - 1) * NS:d * NS],
-                                         dst=dst[:, NV + (d - 1) * NS:NV + d * NS]))
+                                         remote_sem=T.sem[rsem], src=src(d), dst=dst(d)))
             cnt[lsem] = cnt.get(lsem, 0) + len(eng[d])
         g.remote_dma_fused(trs, local_sem=T.sem[lsem])
 
-    HW, AX = [T.HW0, T.HW1], [T.AX0, T.AX1]
+    def block(buf, c0=0):
+        return lambda d: buf[:, c0 + (d - 1) * NS:c0 + d * NS]
+
+    def moved(dst, d0, src, s0, n, k=1):
+        s = 16 * k
+        return [(dst[s:128, d0:d0 + n], src[0:128 - s, s0:s0 + n]), (dst[0:s, d0:d0 + n], src[128 - s:128, s0:s0 + n])]
+
+    HW, AC = [T.HW0, T.HW1], [T.AC0, T.AC1]
     K, N, R = [T.K0, T.K1, T.K2, T.K3], [T.N0, T.N1], [T.R0, T.R1]
     CF = T.CF
-    c_p, c_pm, c_r, c_r7, c_g, c_show, c_mM, c_mL = [CF[:, j:j + 1] for j in range(8)]
+    c_p, c_pm, c_r, c_r4, c_g, c_x, c_4, c_l0, c_m0, c_l1, c_m1, c_rr, c_t, c_ev = [CF[:, j:j + 1] for j in range(14)]
+    OH, RH = 16, 20
 
-    dma("Y", "dM", [(T.MI[:, 0:64], T.mt[:]), (T.MI[:, 64:128], T.mm[:])], w=["MI"])
-    dma("S", "dSN", [(T.LP[0:112, 256:328], T.sn[16:128, :]), (T.LP[112:128, 256:328], T.sn[0:16, :])], w=["SN"])
-    dma("Y", "dHR", [(T.HR[0:112, :], T.h0[16:128, :]), (T.HR[112:128, :], T.h0[0:16, :])], w=["HR0", "HR1", "HR2", "HR3"])
+    IB, W2 = T.IW[:, 0:128], [T.W0, T.W1]
+    dma("S", "dM", [(T.MI[:, 0:64], T.mt[:]), (T.MI[:, 64:128], T.mm[:])], w=["MI"])
+    dma("Y", "dSN", moved(T.LP, 256, T.sn, 0, 72, 7), w=["SN"])
+    dma("Y", "dHR", moved(T.HR, 0, T.h0, 0, NV, 7), w=["HR0", "HR1", "HR2", "HR3"])
+    wait("Y", [lastw["HR0"]])
     dma("Y", "dL", [(T.LP[:, 0:256], T.pd[:]), (T.LB[:], T.lb[:]), (T.OB[:], T.obs[:])], w=["PD", "LB", "OB"])
-    dma("Y", "dW", [(T.W2[:, 0:NA], T.wv[:])], w=["W1"])
+    dma("Y", "dH", [(T.HW0[:, 0:NV], T.h0[:])], w=["HW0o0", "HW0o1", "HW0o2", "HW0o3"])
+    dma("Y", "dW0", [(T.W0[:, 0:NA], T.wv[:])], w=["Wa"])
     op("G", lambda: g.iota(T.PI[:], [[112, 4]], 0, 1), w=["PI"])
+    op("G", lambda: g.iota(T.YI[:], [[0, 2], [1, 128]], 0, 0, allow_small_or_imprecise_dtypes=True), w=["YI"])
+    op("G", lambda: g.iota(T.CC[:], [[1, 64], [64, 4]], 0, 0, allow_small_or_imprecise_dtypes=True), w=["CC"])
     op("G", lambda: g.iota(T.T3[:], [[1, 16], [16, 8]], 0, 0, allow_small_or_imprecise_dtypes=True), w=["T3"])
-    op("G", lambda: g.iota(T.YI[:], [[1, 144]], 0, 0, allow_small_or_imprecise_dtypes=True), w=["YI"])
     op("G", lambda: g.iota(T.CI[:], [[16, 64]], 0, 0), w=["CI"])
     dma("G", "dT", [(T.TH[:, 0:1], T.th[:])], w=["TH"], slow=True)
     op("V", lambda: g.vector.memset(T.UM[:], 0.0), w=["UM"])
-    op("V", ts(T.PJ[:, 0:2], T.PI[:, 0:2], 127, A.bitwise_and), r=["PI"], w=["PJa"])
-    op("V", ts(T.PJ[:, 2:3], T.PI[:, 0:1], 15, A.bitwise_and), r=["PI"], w=["PJb"])
-    op("V", ts(T.PJ[:, 3:4], T.PI[:, 0:1], 7, A.bitwise_and), r=["PI"], w=["PJc"])
-    op("V", cp(CF[:, 0:4], T.PJ[:]), r=["PJa", "PJb", "PJc"], w=["CF"])
-    op("V", [ts(T.UM[:, :, 3:131:16], T.T3[:], c_p, A.is_equal),
-             ts(T.UM[:, :, 11:131:16], T.T3[:], c_pm, A.is_equal)], r=["T3", "CF"], w=["UM"])
-    op("V", ts(c_show, c_r, 8.0, A.is_ge), r=["CF"], w=["c_show"])
-    op("V", ts(c_g, c_p, c_r, A.subtract, 15.0, A.add), r=["CF"], w=["c_g"])
-    op("V", ts(c_mM, c_r7, 3.0, A.is_lt), r=["CF"], w=["c_mM"])
-    op("V", ts(c_mL, c_r7, 3.0, A.is_equal, 4.0, A.mult), r=["CF"], w=["c_mL"])
-    op("V", ts(T.IB[:], T.YI[:, 0:128], c_p, A.is_equal), r=["YI", "CF"], w=["IB"])
+    op("V", [ts(T.PJ[:, 0:2], T.PI[:, 0:2], 127, A.bitwise_and), ts(T.PJ[:, 2:3], T.PI[:, 0:1], 15, A.bitwise_and),
+             ts(T.PJ[:, 3:4], T.PI[:, 0:1], 3, A.bitwise_and)], r=["PI"], w=["PJ"])
+    op("V", cp(CF[:, 0:4], T.PJ[:]), r=["PJ"], w=["CF"])
+    op("V", [ts(c_4, c_r, 4.0, A.is_ge), ts(c_x, c_r, 3.0, A.is_equal)], r=["CF"], w=["c_4"])
+    op("V", ts(T.IW[:], T.YI[:], c_p, A.is_equal), r=["YI", "CF"], w=["IB"])
+    op("V", ts(CF[:, OH:OH + 4], T.YI[:, 0:4], c_r4, A.is_equal, c_4, A.mult), r=["YI", "c_4"], w=["OH"])
+    op("V", ts(T.UM[:, :, 3:131:16], T.T3[:], c_pm, A.is_equal), r=["T3", "CF"], w=["UM"])
+    op("V", [ts(T.SX[:, j:NV:4], T.CC[:], c_x, A.mult, CF[:, OH + j:OH + j + 1], A.add) for j in range(4)], r=["CC", "OH"], w=["SX"])
+    for b in range(2):
+        op("P", mm(N[b][:], IB, T.SX[:, 512 * b:512 * b + 512], True, False), r=["IB", "SX"], w=["N%d" % b], bk=["N%d" % b])
 
     def U(i, row):
         return T.UM[:, i, 3 - row:131 - row]
 
     pcs = [T.PC[:, 64 * j:64 * j + 64] for j in range(4)]
+    op("V", cp(T.ON[:, 256:328], T.LP[:, 256:328]), r=["SN"], w=["ONs"])
     op("V", cp(pcs[0], T.MI[:, 0:64]), r=["MI"], w=["PC0"])
     op("V", ts(T.TI[:, 0:64], T.MI[:, 64:128], 511, A.bitwise_and), r=["MI"], w=["TIa"])
     op("V", tt(pcs[1], T.MI[:, 0:64], pcs[0], A.subtract), r=["MI", "PC0"], w=["PC1"])
     op("V", ts(pcs[3], T.TI[:, 0:64], -256.0, A.add), r=["TIa"], w=["PC3"])
-    op("V", cp(T.ON[:, 256:328], T.LP[:, 256:328]), r=["SN"], w=["ONs"])
+
+    hr_keys = ["HR0", "HR1", "HR2", "HR3"]
+
+    def show(e, j, t=0):
+        c0, c1 = (24 * (far[j] - 1), 24 * far[j]) if j < 2 else (24 * near[0] - 48 + 12 * j, 24 * near[0] - 36 + 12 * j)
+        o = 328 * t + 256
+        op(e, copy(e, T.SH[:, 16 * c0:16 * c1], T.HR[:, 0:NV].indirect(T.ON[:, o + c0:o + c1])), r=hr_keys + ["ONr" if t else "ONs"], w=["SH%d" % j])
+
+    def send_h(t, j):
+        keys = ["SH%d" % (2 * j), "SH%d" % (2 * j + 1)]
+        send(block(T.SH), block(HW[t % 2], NV), [far, near][j], "arrH%d" % t, "locH%d" % j, keys, alone if t == 0 and j else eng)
+        for k in keys:
+            readers.setdefault(k, []).append(("locH%d" % j, cnt["locH%d" % j]))
+        lastw["HW%dr" % (t % 2)] = ("arrH%d" % t, arrive + (0 if t else sum(len(alone[d]) - len(eng[d]) for d in near)))
+
+    show("S", 2)
+    show("V", 3)
+    send_h(0, 1)
     for b in range(2):
         fns = []
         for i in range(8 * b, 8 * b + 8):
             o = N[b][:, 64 * (i % 8):64 * (i % 8) + 64]
-            fns += [mm(o, U(i, 0), pcs[0], True, False), mm(o, U(i, 1), pcs[1], False, False), mm(o, U(i, 3), pcs[3], False, True)]
+            fns += [mm(o, U(i, 0), pcs[0], False, False), mm(o, U(i, 1), pcs[1], False, False), mm(o, U(i, 2), pcs[3], False, i % 8 == 7)]
         op("P", fns, r=["UM", "PC0", "PC1", "PC3"], w=["N%d" % b], bk=["N%d" % b])
-    op("V", lambda: g.vector.memset(T.AX0[:, 0:NV], 0.0), w=["AX0o"])
-    op("V", ts(T.WL[:], T.YI[:], c_g, A.is_equal, c_mL, A.mult), r=["YI", "c_g", "c_mL"], w=["WL"])
-    op("V", ts(T.WM[:], T.YI[:], c_g, A.is_equal, c_mM, A.mult), r=["YI", "c_g", "c_mM"], w=["WM"])
-    op("V", ts(T.WC[:], T.YI[:], c_g, A.is_equal, 16384.0, A.mult), r=["YI", "c_g"], w=["WC"])
-    op("V", ts(T.PF[:], T.YI[:, 0:128], c_pm, A.is_equal), r=["YI", "CF"], w=["PF"])
-
-    hr_keys = ["HR0", "HR1", "HR2", "HR3"]
-
-    def show_h(e, c0, c1, key):
-        src = T.HR[:, 0:NV].indirect(T.ON[:, 256 + c0:256 + c1])
-        o = T.SH[:, 16 * c0:16 * c1]
-        op(e, cp(o, src) if e == "V" else act(o, src, AF.Copy), r=hr_keys + ["ONs"], w=[key])
-
-    def send_h(t):
-        send(T.SH, HW[t % 2], far, "arrH%d" % t, "locH", ["SH%d" % d for d in far])
-        if near:
-            send(T.SH, HW[t % 2], near, "arrH%d" % t, "locH", ["SH%d" % near[0], "SHx"])
-        for k in ["SH1", "SH2", "SH3", "SHx"]:
-            readers.setdefault(k, []).append(("locH", cnt["locH"]))
-        lastw["HW%dr" % (t % 2)] = ("arrH%d" % t, arrive)
-
-    def evac(b):
-        o = T.SW[:, 512 * b:512 * b + 512]
-        op("SV"[b], copy("SV"[b], o, N[b][:]), r=["N%d" % b], w=["SW%d" % b], bk=["N%d" % b])
-
-    def show_a(t):
-        off, key = (T.ON, "ONs") if t == 0 else (T.OP, "OP")
-        p = t % 2
-        dma("Y", "dOwn", [(AX[p][j:128:16, 0:NV], T.SW[j:128:16, :]) for j in range(4)], r=["SW0", "SW1"], w=["AX%do" % p])
-        op("V", ts(T.SA[:, 0:576], T.SW[:, 0:NV].indirect(off[:, 256:292]), c_show, A.mult), r=["SW0", "SW1", key, "c_show"], w=["SA0"])
-        op("S", act(T.SA[:, 576:1152], T.SW[:, 0:NV].indirect(off[:, 292:328]), AF.Identity, scale=c_show),
-           r=["SW0", "SW1", key, "c_show"], w=["SA1"])
-        send(T.SA, AX[p], far + near, "arrA%d" % t, "locA", ["SA0", "SA1"])
-        for k in ["SA0", "SA1"]:
-            readers.setdefault(k, []).append(("locA", cnt["locA"]))
-        lastw["AX%dr" % p] = ("arrA%d" % t, arrive)
-
-    evac(0)
-    evac(1)
-    show_a(0)
-    for d in far + near:
-        show_h("S", 24 * (d - 1), 24 * d, "SH%d" % d)
-    send_h(0)
-    dma("S", "dH", [(T.HW0[:, 0:NV], T.h0[:])], w=["HW0o0", "HW0o1", "HW0o2", "HW0o3"])
+    op("V", [ts(c_g, c_p, c_r, A.subtract, 15.0, A.add), ts(c_l0, c_r, 2.0, A.is_equal, 4.0, A.mult), ts(c_m0, c_r, 2.0, A.is_lt),
+             ts(c_l1, c_r, 12.0, A.is_ge, 4.0, A.mult), ts(c_m1, c_r, 12.0, A.is_lt, c_4, A.mult), ts(c_rr, c_r, c_r4, A.subtract)],
+       r=["CF", "c_4"], w=["c_g"])
+    for b in range(2):
+        op("SV"[b], copy("SV"[b], T.SW[:, 512 * b:512 * b + 512], N[b][:]), r=["N%d" % b], w=["SW%d" % b], bk=["N%d" % b])
+    for b in range(2):
+        op("P", mm(K[b][:], T.IW[:, 112:240], T.SW[:, 512 * b:512 * b + 512], True, True), r=["SW%d" % b], w=["KA%d" % b], bk=["K%d" % b])
+    for b in range(2):
+        op("SV"[b], copy("SV"[b], T.SA[:, 576 * b:576 * b + 576], T.SW[:, 0:NV].indirect(T.ON[:, 256 + 36 * b:292 + 36 * b])),
+           r=["SW0", "SW1", "ONs"], w=["SA%d" % b])
+    send(block(T.SA), block(T.AX, NV), far + near, "arrA0", "locA", ["SA0", "SA1"])
+    lastw["AXr0"] = ("arrA0", arrive)
+    show("S", 0)
+    show("V", 1)
+    send_h(0, 0)
+    op("S", [act(T.AX[:, 512 * b:512 * b + 512], K[b][:], AF.Copy) for b in range(2)], r=["KA0", "KA1"], w=["AXo0"], bk=["K0", "K1"])
 
     op("V", cp(T.ON[:, 0:256], T.LP[:, 0:256]), r=["PD"], w=["ONp"])
+    for w, c in ((T.WL0, c_l0), (T.WM0, c_m0), (T.WL1, c_l1), (T.WM1, c_m1), (T.WX, c_x), (T.WC, 16384.0)):
+        op("V", ts(w[:], T.YI[:, 0:w.shape[1]], c_g, A.is_equal, c, A.mult), r=["YI", "c_g"], w=["WW"])
     for k in range(4):
-        op("V", ts(T.ST[:, k, 0:64], T.LB[:, 64 * k:64 * k + 64], 1024.0 + 4096 * k, A.add), r=["LB"], w=["STa%d" % k])
-        op("V", ts(T.ST[:, k, 64:128], T.LP[:, 64 * k:64 * k + 64], 4096.0 * k, A.add), r=["PD"], w=["STb%d" % k])
-    stk = ["STa%d" % k for k in range(4)] + ["STb%d" % k for k in range(4)]
-    op("S", act(T.SHI[:, :, 0:128], T.ST[:], AF.Copy), r=stk, w=["SHI"])
-    op("V", ts(T.X4[:], T.LP[:], 1023.0, A.min), r=["PD", "SN"], w=["X4"])
-    op("V", ts(T.X3[:], T.LP[:], 1023.0, A.min, 0.9375, A.mult), r=["PD", "SN"], w=["X3"])
-    op("V", ts(T.X1[:], T.X4[:], 15, A.bitwise_and), r=["X4"], w=["X1"])
-    op("V", tt(T.SLO[:], T.ST[:], T.SHI[:, :, 0:128], A.subtract), r=stk + ["SHI"], w=["SLO"])
-    op("S", act(T.I14[:], T.IB[:], AF.Copy, scale=16384.0), r=["IB"], w=["I14"])
-    op("S", act(T.ZB[:], T.IB[:], AF.Copy, scale=0.0), r=["IB"], w=["ZB"])
-    op("S", act(T.O8[:], T.OB[:], AF.Copy, scale=0.125), r=["OB"], w=["O8"])
-    op("S", act(T.W2[:, NA:2 * NA], T.W2[:, 0:NA], AF.Copy), r=["W1"], w=["W2"])
-    op("S", act(T.NTH[:, 0:1], T.TH[:, 0:1], AF.Copy, scale=-1.0), r=["TH"], w=["NTH"])
-    op("S", act(T.IF[:], T.IB[:], AF.Copy), r=["IB"], w=["IF"])
-    op("S", act(T.AX1[:, 0:NV], T.W2[:, 0:NV], AF.Copy, scale=0.0), r=["W1"], w=["AX1o"])
-    op("V", ts(T.X2[:], T.X1[:], 63.9375, A.mult), r=["X1"], w=["X2"])
-    op("V", tt(T.X3[:], T.LP[:], T.X3[:], A.subtract), r=["PD", "SN"], w=["X3"])
+        op("V", [ts(T.ST[:, k, 0:64], T.LB[:, 64 * k:64 * k + 64], 1024.0 + 4096 * k, A.add),
+                 ts(T.ST[:, k, 64:128], T.LP[:, 64 * k:64 * k + 64], 4096.0 * k, A.add)], r=["LB", "PD"], w=["ST%d" % k])
+    stk = ["ST%d" % k for k in range(4)]
+    op("S", act(T.SHI[:], T.ST[:], AF.Copy), r=stk, w=["SHI"])
+    op("V", [ts(T.DD[:, j, :], T.LP[:, 0:256], float(NV + NS * j), A.is_ge, float(NC), A.mult) for j in range(3)], r=["PD"], w=["DD"])
+    op("V", [ts(c_t, c_pm, c_rr, A.subtract, c_r4, A.subtract), ts(CF[:, RH:RH + 4], T.YI[:, 0:16:4], c_rr, A.is_equal),
+             ts(c_ev, c_rr, 8.0, A.is_equal, -192.0, A.mult)], r=["c_g"], w=["c_t"])
+    op("V", tt(T.SLO[:], T.ST[:], T.SHI[:], A.subtract), r=stk + ["SHI"], w=["SLO"])
+    op("V", ts(c_t, c_t, c_r4, A.add, 12.0, A.add), r=["c_t"], w=["c_t"])
     op("V", ts(T.VI[:], T.CI[:], c_r, A.add), r=["CI", "CF"], w=["VI"])
+    op("V", [ts(T.CM[:, j, :], T.YI[:, 0:168], c_t, A.is_equal, CF[:, RH + j:RH + j + 1], A.mult) for j in range(4)], r=["c_t"], w=["CM"])
+    op("S", [act(T.CB[:, 0:4], T.OB[:], AF.Copy), act(T.CB[:, 4:8], T.OB[:], AF.Copy, scale=0.125),
+             act(T.CB[:, 8:9], T.TH[:, 0:1], AF.Copy), act(T.CB[:, 9:10], T.TH[:, 0:1], AF.Copy, scale=-1.0)], r=["OB", "TH"], w=["CB"])
+    op("S", act(T.I14[:], IB, AF.Copy, scale=16384.0), r=["IB"], w=["I14"])
+    op("S", act(T.ZB[:], IB, AF.Copy, scale=0.0), r=["IB"], w=["ZB"])
+    op("S", act(T.W0[:, NA:2 * NA], T.W0[:, 0:NA], AF.Copy), r=["Wa"], w=["W0"])
+    op("S", act(T.IF[:], IB, AF.Copy), r=["IB"], w=["IF"])
 
-    def late_constants(j):
-        op("V", tt(T.X1[:], T.X2[:], T.X3[:], A.add), r=["X2", "X3"], w=["X1"])
-        op("V", cp(T.OP[:], T.X1[:]), r=["X1"], w=["OP"])
+    def shifted(w, c0, t=0):
+        c = (c0 - 16 * t) % 128
+        return w[:, c:c + 128]
 
-    def wrap(out, w, src, k, last, first=False):
-        return [mm(out, w[:, 15 - i:143 - i], src[:, 1024 * k + i:1024 * k + 1024:16], first and i == 0, last and i == 15) for i in range(16)]
+    def wrap(out, w, src, k, last, first=False, t=0):
+        return [mm(out, shifted(w, 15 - i, t), src[:, 1024 * k + i:1024 * k + 1024:16], first and i == 0, last and i == 15) for i in range(16)]
 
-    def ps_a(k):
-        return R[k % 2][:, 128 * (k // 2):128 * (k // 2) + 64]
+    turn = {}
+
+    def bank_a(js, new=False):
+        if new:
+            turn["n"] = 1 - turn.get("n", 1)
+            turn.update((j, "R%d" % turn["n"]) for j in js)
+        return turn[js[0]]
+
+    def ps_a(js):
+        return T[bank_a(js)][:, 32 * js[0]:32 * js[-1] + 32]
 
     def ps_m(k):
         return N[k // 2][:, 64 * (k % 2):64 * (k % 2) + 64]
 
     def ps_b(k):
-        return R[0][:, 256:320] if k == 3 else K[k][:, 64:128]
+        return R[0][:, 128 + 64 * k:192 + 64 * k] if k >= 2 else K[k][:, 64:128]
 
-    for t in range(NT):
+    def names(kind, js):
+        return ["%s%d" % (kind, j) for j in js]
+
+    def step(t):
         p, q = t % 2, (t + 1) % 2
         last = t == NT - 1
-        off, okey = (T.ON, "ONp") if t == 0 else (T.OP, "OP")
+        AG, WL, WM = (T.MK, T.WL0, T.WM0) if t == 0 else (T.AG, T.WL1, T.WM1)
+        ag = "MK" if t == 0 else "AG"
         hwk = ["HW%do%d" % (p, j) for j in range(4)] + ["HW%dr" % p]
-        y, y8 = T.OB[:, t:t + 1], T.O8[:, t:t + 1]
+        y, y8, th, nth = [T.CB[:, 16 * t + j:16 * t + j + 1] for j in (t, 4 + t, 8, 9)]
+        cb, on, IT = "ONr" if t else "CB", "ONr" if t else "ONp", shifted(T.IW, 0, t)
+        KA, KB = T.KI[:, 0:64], T.KI[:, 64:128]
+        CH = CH_LAST if last else CH_STEP
+        two = lambda kind, k: names(kind, (2 * k, 2 * k + 1))
 
-        def sl(buf, j):
-            return buf[:, 512 * j:512 * j + 512]
+        def sl(buf, js, n=512):
+            return buf[:, n * js[0]:n * js[-1] + n]
 
-        def aux(e, j):
-            src = AX[p][:, 0:NW].indirect(off[:, 32 * j:32 * j + 32])
-            op(e, copy(e, sl(T.AG, j), src),
-               r=["AX%do" % p, "AX%dr" % p, okey], w=["AG%d" % j])
+        def aux(e, js):
+            if t == 0:
+                op(e, copy(e, sl(T.MK, js), T.AX[:, 0:NW].indirect(sl(T.ON, js, 32))), r=["AXo0", "AXr0", "ONp"], w=names("MK", js))
+            else:
+                op("V", tt(sl(T.AG, js), AC[p][:, 0:NR * NC].indirect(sl(T.OC, js, 32)), sl(T.MK, js), A.mult),
+                   r=["AXo%d" % t, "AXr%d" % t, "OC"] + names("MK", js), w=names("AG", js))
 
-        def mwrap(k):
-            o = ps_a(k)
-            op("P", [mm(o, T.IB[:], T.SHI[:, k, 0:64], True, False), mm(o, T.IB[:], T.SLO[:, k, 0:64], False, False)]
-               + wrap(o, T.WL, T.AG, k, True),
-               r=["IB", "SHI", "SLO", "WL", "AG%d" % (2 * k), "AG%d" % (2 * k + 1)], w=["PA%d" % k], bk=["R%d" % (k % 2)])
+        def mwrap(e, js):
+            bank_a(js, True)
+            o, k, c0, c1 = ps_a(js), js[0] // 2, 32 * (js[0] % 2), 32 * (js[-1] % 2) + 32
+            op("P", [mm(o, IT, T.SHI[:, k, c0:c1], True, False), mm(o, IT, T.SLO[:, k, c0:c1], False, False)]
+               + [mm(o, shifted(WL, 15 - i, t), AG[:, 512 * js[0] + i:512 * js[-1] + 512:16], False, i == 15) for i in range(16)],
+               r=["IB", "SHI", "SLO", "WW"] + names(ag, js), w=names("PA", js), bk=[bank_a(js)])
 
-        def conv(k):
-            op("V", ts(T.OA[:, 64 * k:64 * k + 64], ps_a(k), -4096.0 * k, A.add), r=["PA%d" % k], w=["OA%d" % k], bk=["R%d" % (k % 2)])
+        def conv(e, js):
+            op("V", ts(sl(T.OA, js, 32), ps_a(js), -4096.0 * (js[0] // 2), A.add), r=names("PA", js), w=names("OA", js), bk=[bank_a(js)])
 
-        def Mwrap(k):
-            op("P", wrap(ps_m(k), T.WM, T.AG, k, True, first=True), r=["WM", "AG%d" % (2 * k), "AG%d" % (2 * k + 1)],
-               w=["KM%d" % k], bk=["N%d" % (k // 2)])
+        def Mwrap(e, k):
+            op("P", wrap(ps_m(k), WM, AG, k, True, True, t), r=["WW"] + two(ag, k), w=["KM%d" % k], bk=["N%d" % (k // 2)])
 
-        def keys(k):
-            n = 64 if k == 3 else 128
+        def keys(e, k):
+            n = 64 if k >= 2 else 128
             o = K[k][:, 0:n]
-            op("P", [mm(o, T.IB[:], T.SHI[:, k, 0:n], True, False), mm(o, T.IB[:], T.SLO[:, k, 0:n], False, False)]
-               + wrap(K[k][:, 0:64], T.WL, T.AG, k, False),
-               r=["IB", "SHI", "SLO", "WL", "AG%d" % (2 * k), "AG%d" % (2 * k + 1)], w=["KA%d" % k, "KB%d" % k], bk=["K%d" % k])
+            op("P", [mm(o, IT, T.SHI[:, k, 0:n], True, False), mm(o, IT, T.SLO[:, k, 0:n], False, False)]
+               + wrap(K[k][:, 0:64], WL, AG, k, False, False, t),
+               r=["IB", "SHI", "SLO", "WW"] + two(ag, k), w=["KA%d" % k, "KB%d" % k], bk=["K%d" % k])
 
-        def wa(e, j):
-            src = T.W2[:, 0:4096].indirect(T.OA[:, 32 * j:32 * j + 32])
-            op(e, copy(e, sl(T.WA, j), src), r=["W2", "OA%d" % (j // 2)], w=["WA%d" % j])
+        def xwrap(e, j):
+            fns = [mm(R[1][:, 256:512], IB, T.DD[:, i, :], i == 0, False) for i in range(3)]
+            for k in range(4):
+                fns += wrap(R[1][:, 256 + 64 * k:320 + 64 * k], T.WX, T.MK, k, k == 3)
+            op("P", fns, r=["IB", "DD", "WW"] + names("MK", range(8)), w=["PX"], bk=["R1"])
+
+        def xconv(e, j):
+            op("V", cp(T.OC[:], R[1][:, 256:512]), r=["PX"], w=["OC"], bk=["R1"])
+
+        def wa(e, js):
+            op(e, copy(e, sl(T.WA, js), W2[p][:, 0:4096].indirect(sl(T.OA, js, 32))), r=["W%d" % p] + names("OA", js), w=names("WA", js))
+
+        def loads(e, j):
+            wait("Y", [lastw["PR0"]])
+            if t == 0:
+                dma("Y", "dR", [x for u in range(1, NT) for x in moved(T.ON, 328 * u, T.ON, 0, 328, u) + moved(T.CB, 16 * u, T.CB, 0, 10, u)],
+                    r=["ONs", "ONp", "CB"], w=["ONr"])
+            dma("Y", "dW%d" % (t + 1), moved(W2[q], 0, T.wv, 0, NA, t + 1) + moved(W2[q], NA, T.wv, 0, NA, t + 1), w=["W%d" % q])
 
         def least(e, j):
             if j == 0:
@@ -320,177 +375,179 @@ def rank_program(g, core, T, topo):
         def addrel(e, k):
             rl = T.RL[:, 64 * k:64 * k + 64]
             fns = [mm(K[k][:, 0:64], T.I14[:], rl, False, False)]
-            if k == 3:
-                fns += [mm(ps_b(3), T.IB[:], T.SHI[:, 3, 64:128], True, False), mm(ps_b(3), T.IB[:], T.SLO[:, 3, 64:128], False, False)]
+            if k == 2:
+                fns += [mm(R[0][:, 256:384], T.ZB[:], T.CC[:, 0:128], True, False)]
+            if k >= 2:
+                fns += [mm(ps_b(k), IT, T.SHI[:, k, 64:128], False, False), mm(ps_b(k), IT, T.SLO[:, k, 64:128], False, False)]
             op("P", fns + [mm(ps_b(k), T.I14[:], rl, False, False)],
-               r=["I14", "RL%d" % k], w=["KA%d" % k, "KB%d" % k], bk=["K%d" % k] + (["R0"] if k == 3 else []))
+               r=["I14", "ZB", "RL%d" % k], w=["KA%d" % k, "KB%d" % k], bk=["K%d" % k] + (["R0"] if k >= 2 else []))
 
         def split(e, j):
             if last:
-                if j == 1:
-                    op("V", ts(T.MF[:], T.MN[:], -192.0 * (NT - 1), A.add), r=["MN"], w=["MF"])
-            elif j == 0:
+                return
+            if j == 0:
                 op(e, copy(e, pcs[0], T.MN[:]), r=["MN"], w=["PC0"])
             else:
                 op("V", tt(pcs[1], T.MN[:], pcs[0], A.subtract), r=["MN", "PC0"], w=["PC1"])
 
-        def unwrap1(e, b):
-            if last:
-                return
-            fns = [mm(N[b][:], T.ZB[:], T.W2[:, 0:512], True, False)]
-            for i in range(8 * b, 8 * b + 8):
-                o = N[b][:, 64 * (i % 8):64 * (i % 8) + 64]
-                fns += [mm(o, U(i, 0), pcs[0], False, False), mm(o, U(i, 1), pcs[1], False, False)]
-            op("P", fns, r=["UM", "ZB", "W2", "PC0", "PC1"], w=["N%d" % b], bk=["N%d" % b])
+        def compact(pairs, stop):
+            return [mm(N[0][:, 64 * rh:64 * rh + 64], T.CM[:, rh, 8 - 4 * j + 16 * t:136 - 4 * j + 16 * t], pcs[i], False, stop and rh == 3 and n == 1)
+                    for rh in range(4) for n, (i, j) in enumerate(pairs)]
 
-        def prod(j):
-            op("V", tt(sl(T.PR, j), HW[p][:, 0:NW].indirect(T.ON[:, 32 * j:32 * j + 32]), sl(T.WA, j), A.mult),
-               r=hwk + ["ONp", "WA%d" % j], w=["PR%d" % j])
-
-        def absd(j):
-            op("S", act(sl(T.RR, j), sl(T.PR, j), AF.Abs, bias=y, scale=-1.0), r=["PR%d" % j, "OB"], w=["RR%d" % j])
-
-        def gt(j):
-            op("V", ts(sl(T.FL, j), sl(T.RR, j), T.TH[:, 0:1], A.is_gt), r=["RR%d" % j, "TH"], w=["FL%d" % j])
-
-        def helpgt(j):
-            op("S", act(sl(T.FL, j), sl(T.RR, j), AF.Sign, bias=T.NTH[:, 0:1]), r=["RR%d" % j, "NTH"], w=["FL%d" % j])
-            op("S", act(sl(T.FL, j), sl(T.FL, j), AF.Relu), w=["FL%d" % j])
-
-        def count(k, which):
-            o = K[k][:, 0:64] if which == "A" else ps_b(k)
-            op("P", wrap(o, T.WC, T.FL, k, which == "B" or k == 3), r=["WC", "FL%d" % (2 * k), "FL%d" % (2 * k + 1)],
-               w=["K%s%d" % (which, k)], bk=["R0" if which == "B" and k == 3 else "K%d" % k])
-
-        def best(e, k):
-            src = K[k][:, 0:128]
-            op(e, copy(e, T.BE[:], src) if k == 0 else tt(T.BE[:], T.BE[:], src, A.min), r=["KA%d" % k, "KB%d" % k], w=["BE"], bk=["K%d" % k])
-
-        def counts(e, k):
-            count(k, "A")
-            count(k, "B")
+        def early(e, j):
+            if not last:
+                op("P", [mm(N[0][:, 0:NC], T.ZB[:], T.CC[:], True, False)] + compact([(0, 0), (1, 1)], False),
+                   r=["CM", "ZB", "PC0", "PC1"], w=["N0", "KM0", "KM1"], bk=["N0"])
 
         def late(e, j):
-            if t == 0:
-                late_constants(j)
+            op("P", compact([(2, 1), (3, 2)], True), r=["CM", "PC2", "PC3"], w=["N0"], bk=["N0"])
 
-        make = {"x": aux, "c": lambda e, k: conv(k), "w": wa, "m": least, "r": rel, "l": split, "b": best, "o": late,
-                "p": lambda e, j: prod(j), "a": lambda e, j: absd(j), "g": lambda e, j: gt(j) if e == "V" else helpgt(j),
-                "A": lambda e, k: mwrap(k), "M": lambda e, k: Mwrap(k), "K": lambda e, k: keys(k), "E": addrel, "Z": unwrap1, "C": counts}
+        def evac(e, j):
+            o, i = T.SC[:], N[0][:, 0:NC]
+            op(e, ts(o, i, c_ev, A.add) if e == "V" else act(o, i, AF.Identity, bias=c_ev), r=["N0", "c_t"], w=["SC"], bk=["N0"])
+            dma("Y", "dOwn", moved(AC[q], 0, T.SC, 0, NC), r=["SC"], w=["AXo%d" % (t + 1)])
 
-        def needs(x):
-            kind, j = x[0], int(x[1])
-            two = ["%s%d" % ({"A": "x", "M": "x", "K": "x", "C": "g"}.get(kind, ""), 2 * j + n) for n in range(2)]
-            return {"x": [], "o": [], "A": two, "M": two, "K": two, "c": ["A%d" % j], "w": ["c%d" % (j // 2)],
-                    "m": [["M0", "M1"], ["m0", "M2", "M3"], ["m1"]][min(j, 2)], "r": ["m2"], "l": ["m2"] if j == 0 else ["l0"],
-                    "E": ["r%d" % j, "K%d" % j] + (["c0", "c2"] if j == 3 else []), "Z": ["l1", "r0", "r1", "r2", "r3"],
-                    "p": ["w%d" % j], "a": ["p%d" % j], "g": ["a%d" % j], "C": two + ["E%d" % j],
-                    "b": ["C%d" % j] + (["b%d" % (j - 1)] if j else [])}[kind]
+        def sends(e, j):
+            if j == 0:
+                send(lambda d: T.SC[:], lambda d: AC[q][:, NC * d:NC * d + NC], far + near, "arrA%d" % (t + 1), "locA", ["SC"])
+                readers["SC"].append(("locA", cnt["locA"]))
+                lastw["AXr%d" % (t + 1)] = ("arrA%d" % (t + 1), arrive)
+            else:
+                send_h(t + 1, j - 1)
 
-        todo, made = {e: ORDER[e].split() for e in "VSP"}, set()
-        while any(todo.values()):
-            moved = False
-            for e in "VSP":
-                while todo[e] and all(n in made for n in needs(todo[e][0])):
-                    x = todo[e].pop(0)
-                    make[x[0]](e, int(x[1]))
-                    made.add(x)
-                    moved = True
-            if not moved:
-                raise ValueError("the orders of the queues don't fit")
+        def prod(e, js):
+            op("V", tt(sl(T.PR, js), HW[p][:, 0:NW].indirect(T.ON[:, 328 * t + 32 * js[0]:328 * t + 32 * js[-1] + 32]), sl(T.WA, js), A.mult),
+               r=hwk + [on] + names("WA", js), w=names("PR", js))
 
-        KA, KB = T.KI[:, 0:64], T.KI[:, 64:128]
-        op("V", tt(KA, T.BE[:, 0:64], K[3][:, 0:64], A.min), r=["BE", "KA3"], w=["KIa"], bk=["K3"])
-        if not last:
-            op("V", ts(T.TI[:, 0:64], KA, 511, A.bitwise_and), r=["KIa"], w=["TIa"])
-            op("V", ts(pcs[2], KA, 2.0 ** -14, A.mult, 191.5 + 2.0 ** -15, A.add), r=["KIa"], w=["PC2"])
-            op("V", ts(pcs[3], T.TI[:, 0:64], -256.0, A.add), r=["TIa"], w=["PC3"])
-            for b in range(2):
-                fns = []
-                for i in range(8 * b, 8 * b + 8):
-                    o = N[b][:, 64 * (i % 8):64 * (i % 8) + 64]
-                    fns += [mm(o, U(i, 2), pcs[2], False, False), mm(o, U(i, 3), pcs[3], False, i % 8 == 7)]
-                op("P", fns, r=["UM", "PC2", "PC3"], w=["N%d" % b], bk=["N%d" % b])
-        op("V", ts(T.TI[:, 64:128], KA, 2, A.logical_shift_right, 3072, A.bitwise_and), r=["KIa"], w=["TIb"])
-        if last:
-            op("V", ts(T.MI[:, 0:64], KA, 14, A.logical_shift_right), r=["KIa"], w=["MI", "MIa"])
-            op("V", ts(T.MI[:, 64:128], KA, 2047, A.bitwise_and), r=["KIa"], w=["MIb"])
-        op("V", tt(KB, T.BE[:, 64:128], ps_b(3), A.min), r=["BE", "KB3"], w=["KIb"], bk=["R0"])
-        op("V", tt(T.OI[:, 128:192], T.TI[:, 64:128], T.VI[:], A.add), r=["TIb", "VI"], w=["OIb"])
-        op("V", ts(T.OI[:, 0:128], T.KI[:], 4095, A.bitwise_and), r=["KIa", "KIb"], w=["OIa"])
-        op("V", cp(T.OS[:], T.OI[:]), r=["OIa", "OIb"], w=["OS"])
+        def absd(e, js):
+            op("S", act(sl(T.RR, js), sl(T.PR, js), AF.Abs, bias=y, scale=-1.0), r=names("PR", js) + [cb], w=names("RR", js))
 
-        prk = ["PR%d" % j for j in range(8)]
-        CH = CH_LAST if last else CH_STEP
+        def gt(e, js):
+            if e == "V":
+                op("V", ts(sl(T.FL, js), sl(T.RR, js), th, A.is_gt), r=names("RR", js) + [cb], w=names("FL", js))
+            else:
+                op("S", act(sl(T.FL, js), sl(T.RR, js), AF.Sign, bias=nth), r=names("RR", js) + [cb], w=names("FL", js))
+                op("S", act(sl(T.FL, js), sl(T.FL, js), AF.Relu), w=names("FL", js))
 
-        def c4(buf, j):
-            return buf[:, 16 * CH[j]:16 * CH[j + 1]]
+        def half(e, j, odd):
+            o, i, key = T.FL[:, 512 * j + odd:512 * j + 512:2], T.RR[:, 512 * j + odd:512 * j + 512:2], "F%d%d" % (odd, j)
+            if e == "V":
+                op("V", ts(o, i, th, A.is_gt), r=["RR%d" % j, cb], w=[key])
+            else:
+                op("S", act(o, i, AF.Sign, bias=nth), r=["RR%d" % j, cb], w=[key])
+                op("S", act(o, o, AF.Relu), w=[key])
 
-        def o4(c0, j):
-            return T.OS[:, c0 + CH[j]:c0 + CH[j + 1]]
+        def counts(e, k):
+            if k < 2:
+                for which, o in (("A", K[k][:, 0:64]), ("B", ps_b(k))):
+                    op("P", wrap(o, T.WC, T.FL, k, which == "B"), r=["WW"] + two("FL", k), w=["K%s%d" % (which, k)], bk=["K%d" % k])
+            elif k == 2:
+                op("P", wrap(K[2][:, 0:64], T.WC, T.FL, 2, True), r=["WW"] + two("FL", 2), w=["KA2"], bk=["K2"])
+            elif k < 5:
+                op("P", wrap(K[3][:, 0:64], T.WC, T.FL, 3, True)[k - 3::2], r=["WW", "F%d6" % (k - 3), "F%d7" % (k - 3)], w=["KA3"], bk=["K3"])
+            else:
+                op("P", wrap(ps_b(k - 3), T.WC, T.FL, k - 3, k == 6), w=["KB%d" % (k - 3)], bk=["R0"])
 
-        def es(j):
-            op("S", act(c4(T.ES, j), T.PR[:, 0:4096].indirect(o4(128, j)), AF.Identity, bias=y8, scale=-0.125),
-               r=prk + ["OS", "O8"], w=["ES%d" % j])
+        def best(e, k):
+            o, src, bank = [(T.BE[:], K[0][:, 0:128], "K0"), (T.BE[:], K[1][:, 0:128], "K1"),
+                            (T.BE[:, 0:64], K[2][:, 0:64], "K2"), (T.BE[:, 64:128], ps_b(2), "R0")][k]
+            op(e, copy(e, o, src) if k == 0 else tt(o, o, src, A.min), r=["KA%d" % k, "KB%d" % k] if k < 2 else ["K%s2" % "AB"[k - 2]],
+               w=["BEa", "BEb"] if k < 2 else ["BE" + "ab"[k - 2]], bk=[bank])
 
-        def uu(j):
-            op("V", tt(c4(T.UU, j), T.W2[:, 0:4096].indirect(o4(0, j)), c4(T.ES, j), A.mult), r=["W2", "OS", "ES%d" % j], w=["UU%d" % j])
+        def survivors(e, j):
+            TA, TB, OA, OB = T.TI[:, 0:64], T.TI[:, 64:128], T.OI[:, 0:64], T.OI[:, 64:128]
+            fn, r, w, bk = [
+                (tt(KA, T.BE[:, 0:64], K[3][:, 0:64], A.min), ["BEa", "KA3"], "KIa", ["K3"]),
+                (ts(TA, KA, 2047 if last else 511, A.bitwise_and), ["KIa"], "TIa", []),
+                (ts(T.MI[:, 0:64], KA, 14, A.logical_shift_right) if last else ts(pcs[2], KA, 2.0 ** -14, A.mult, 191.5 + 2.0 ** -15, A.add),
+                 ["KIa"], "PC2", []),
+                (ts(pcs[3], TA, -256.0, A.add), ["TIa"], "PC3", []),
+                (ts(TB, KA, 2, A.logical_shift_right, 3072, A.bitwise_and), ["KIa"], "TIb", []),
+                (tt(OA, TB, T.VI[:], A.add), ["TIb", "VI"], "OIa", []),
+                (cp(T.OS[:, 0:64], OA), ["OIa"], "OSa", []),
+                (tt(KB, T.BE[:, 64:128], ps_b(3), A.min), ["BEb", "KB3"], "KIb", ["R0"]),
+                (ts(OB, KB, 4095, A.bitwise_and), ["KIb"], "OIb", []),
+                (cp(T.OS[:, 64:128], OB), ["OIb"], "OSb", [])][j]
+            op("V", fn, r=r, w=[w], bk=bk)
 
-        def hn(j):
-            op("V", tt(c4(HW[q], j), HW[p][:, 0:NW].indirect(o4(64, j)), c4(T.UU, j), A.add),
-               r=hwk + ["OS", "UU%d" % j], w=["HW%do%d" % (q, j)])
+        def c4(buf, js):
+            return buf[:, 16 * CH[js[0]]:16 * CH[js[-1] + 1]]
+
+        def o4(c0, js):
+            return T.OS[:, c0 + CH[js[0]]:c0 + CH[js[-1] + 1]]
+
+        def es(e, js):
+            src = T.PR[:, 0:4096].indirect(o4(0, js))
+            op(e, act(c4(T.ES, js), src, AF.Identity, bias=y8, scale=-0.125) if e == "S" else ts(c4(T.ES, js), src, -0.125, A.mult, y8, A.add),
+               r=names("PR", range(8)) + ["OSa", cb], w=names("ES", js))
+
+        def uu(e, js):
+            op("V", tt(c4(T.UU, js), T.WA[:, 0:4096].indirect(o4(0, js)), c4(T.ES, js), A.mult),
+               r=names("WA", range(8)) + ["OSa"] + names("ES", js), w=names("UU", js))
+
+        def hn(e, js):
+            op("V", tt(c4(T.HR, js), HW[p][:, 0:NW].indirect(o4(64, js)), c4(T.UU, js), A.add), r=hwk + ["OSb"] + names("UU", js), w=names("HR", js))
+
+        def keep(e, js):
+            c0, n = 16 * CH[js[0]], 16 * (CH[js[-1] + 1] - CH[js[0]])
             if last:
-                dma("S", "dO", [(c4(T.yh, j), c4(HW[q], j))], r=["HW%do%d" % (q, j)])
-                return
-            op("P", mm(K[j][:, 0:16 * (CH[j + 1] - CH[j])], T.PF[:], c4(HW[q], j), True, True), r=["PF", "HW%do%d" % (q, j)], w=["R%d" % j], bk=["K%d" % j])
+                dma("Y", "dO", moved(T.yh, c0, T.HR, c0, n, 8 - t), r=names("HR", js))
+            else:
+                for k in names("HW%do" % q, js):
+                    lastw.pop(k, None)
+                dma("Y", "dOH", moved(HW[q], c0, T.HR, c0, n), r=names("HR", js), w=names("HW%do" % q, js))
 
-        def rot(j):
-            op("S", act(c4(T.HR, j), K[j][:, 0:16 * (CH[j + 1] - CH[j])], AF.Copy), r=["R%d" % j], w=["HR%d" % j], bk=["K%d" % j])
+        def final(e, j):
+            if j == 0:
+                op("V", [tt(T.FO[:, 0:64], T.MI[:, 0:64], T.MN[:], A.add), cp(T.FO[:, 64:128], T.TI[:, 0:64])], r=["PC2", "TIa", "MN"], w=["FO"])
+            elif j == 1:
+                op("P", [(lambda i=i: g.tensor.transpose(N[0][0:32, 128 * i:128 * i + 128], T.FO[:, i:128:4], T.IF[:])) for i in range(4)],
+                   r=["FO", "IF"], w=["N0"], bk=["N0"])
+            else:
+                op("S", [act(T.FT[:, :, i, :], N[0][0:32, 128 * i:128 * i + 128], AF.Copy) for i in range(4)], r=["N0"], w=["FT"], bk=["N0"])
+                dma("S", "dOut", [(T.ymt[gg, :], T.FT[0:16, (gg + t) % 8]) for gg in range(8)]
+                    + [(T.ymm[gg, :], T.FT[16:32, (gg + t) % 8]) for gg in range(8)], r=["FT"])
 
-        if not last:
-            evac(0)
-            evac(1)
-            es(0)
-            show_a(t + 1)
-            es(1)
-            uu(0)
-            uu(1)
-            es(2)
-            hn(0)
-            es(3)
-            uu(2)
-            hn(1)
-            rot(0)
-            uu(3)
-            rot(1)
-            hn(2)
-            hn(3)
-            rot(2)
-            rot(3)
-            show_h("V", 24 * (far[0] - 1), 24 * far[0], "SH%d" % far[0])
-            show_h("S", 24 * (far[1] - 1), 24 * far[1], "SH%d" % far[1])
-            c0 = 24 * (near[0] - 1)
-            show_h("V", c0, c0 + 12, "SH%d" % near[0])
-            show_h("S", c0 + 12, c0 + 24, "SHx")
-            send_h(t + 1)
-        else:
-            es(0)
-            op("V", tt(T.FO[:, 0:64], T.MI[:, 0:64], T.MF[:], A.add), r=["MIa", "MF"], w=["FOa"])
-            op("V", cp(T.FO[:, 64:128], T.MI[:, 64:128]), r=["MIb"], w=["FOb"])
-            es(1)
-            uu(0)
-            op("P", lambda: g.tensor.transpose(N[0][:, 0:128], T.FO[:], T.IF[:]), r=["FOa", "FOb", "IF"], w=["N0"], bk=["N0"])
-            op("S", act(T.FT[:], N[0][:, 0:128], AF.Copy), r=["N0"], w=["FT"], bk=["N0"])
-            dma("Y", "dOut", [(T.ymt[gg, :], T.FT[0:64, 16 * gg:16 * gg + 16]) for gg in range(8)]
-                + [(T.ymm[gg, :], T.FT[64:128, 16 * gg:16 * gg + 16]) for gg in range(8)], r=["FT"])
-            es(2)
-            es(3)
-            uu(1)
-            hn(0)
-            uu(2)
-            hn(1)
-            uu(3)
-            hn(2)
-            hn(3)
+        return {"x": aux, "w": wa, "p": prod, "a": absd, "g": gt, "A": mwrap, "c": conv, "M": Mwrap, "K": keys, "r": rel, "E": addrel,
+                "i": lambda e, j: half(e, j, 0), "j": lambda e, j: half(e, j, 1),
+                "C": counts, "b": best, "m": least, "l": split, "Z": early, "Y": late, "v": evac, "n": survivors, "X": xwrap, "o": xconv,
+                "e": es, "u": uu, "h": hn, "k": keep, "s": lambda e, j: show(e, j, t + 1), "t": sends, "f": final,
+                "L": loads if not last else lambda e, j: None}
+
+    def needs(kind, j):
+        two = lambda k: names(k, (2 * j, 2 * j + 1))
+        return {"x": ["-t0", "-o0"], "A": ["x%d" % j], "M": two("x") + ["-v0"], "K": two("x") + ["-n0", "-n7"], "L": ["p0"], "c": ["A%d" % j],
+                "w": ["c%d" % j, "-u3"], "m": [["M0", "M1"], ["m0", "M2", "M3"], ["m1"]][min(j, 2)], "r": ["m2"],
+                "l": ["m2"] if j == 0 else ["l0"], "E": ["r%d" % j, "K%d" % j] + (names("c", range(8)) if j == 2 else ["E2"] if j == 3 else []),
+                "i": ["a%d" % j], "j": ["a%d" % j], "Z": ["l1", "r0", "r1"], "p": ["w%d" % j, "-t1", "-t2", "-e3", "-k3"], "a": ["p%d" % j], "g": ["a%d" % j],
+                "C": two("g") + ["E%d" % j] if j < 3 else ["E3", "i6", "i7"] if j == 3 else ["C%d" % (j - 1), "j6", "j7"],
+                "b": [["C0"], ["C1", "b0"], ["C2", "b1"], ["C6", "b1"]][min(j, 3)], "X": names("x", range(8)) + names("c", range(8)), "o": ["X0"],
+                "n": ["b2", "C4"] if j == 0 else ["b3"] if j == 7 else ["n%d" % {2: 0, 3: 1, 4: 0}.get(j, j - 1)],
+                "Y": ["n2", "n3", "Z0"], "v": ["Y0"], "e": ["n6"], "u": ["e%d" % j], "h": ["u%d" % j, "n9"], "k": ["h%d" % j], "s": names("h", range(4)) + ["L0"],
+                "t": [["v0"], ["s0", "s1"], ["s2", "s3"]][min(j, 2)], "f": ["n1", "n2"] if j == 0 else ["f%d" % (j - 1)]}[kind]
+
+    steps = [step(t) for t in range(NT)]
+    todo = {e: [] for e in "VSPG"}
+    for t in range(NT):
+        for part in (MAIN0 if t == 0 else MAIN, LAST if t == NT - 1 else TAIL):
+            for e in todo:
+                todo[e] += [(t, x) for x in part[e].split()]
+    planned = {(t, x[0] + str(j)) for e in todo for t, x in todo[e] for j in range(int(x[1]), int(x[-1]) + 1)}
+    made = set()
+    while any(todo.values()):
+        progress = False
+        for e in todo:
+            while todo[e]:
+                t, x = todo[e][0]
+                js = list(range(int(x[1]), int(x[-1]) + 1))
+                want = [(t - 1, n[1:]) if n[0] == "-" else (t, n) for j in js for n in needs(x[0], j)]
+                if not all(n in made or n not in planned for n in want):
+                    break
+                todo[e].pop(0)
+                steps[t][x[0]](e, js if x[0] in "xwpagAceuhk" else js[0])
+                made.update((t, x[0] + str(j)) for j in js)
+                progress = True
+        if not progress:
+            raise ValueError("the orders of the queues don't fit")
 
     wait("G", [(s, c) for s, c in cnt.items()])

@@ -11,17 +11,17 @@ SCRATCH = {
     "HR": ("sbuf", [128, NV], F), "SW": ("sbuf", [128, NV], B), "SX": ("sbuf", [128, NV], B), "SC": ("sbuf", [128, NC], B),
     "SH": ("sbuf", [128, 1152], F), "SA": ("sbuf", [128, 1152], B),
     "ES": ("sbuf", [128, NV], F), "UU": ("sbuf", [128, NV], F),
-    "UM": ("sbuf", [128, 16, 132], B), "CM": ("sbuf", [128, 4, 168], B),
+    "UM": ("sbuf", [128, 8, 132], B), "CM": ("sbuf", [128, 4, 168], B),
     "WC": ("sbuf", [128, 144], B), "WX": ("sbuf", [128, 144], B),
     "WM0": ("sbuf", [128, 144], B), "WL0": ("sbuf", [128, 144], B), "WM1": ("sbuf", [128, 256], B), "WL1": ("sbuf", [128, 256], B),
     "IW": ("sbuf", [128, 256], B), "I14": ("sbuf", [128, 128], B), "ZB": ("sbuf", [128, 128], B),
-    "IF": ("sbuf", [128, 128], F),
-    "YI": ("sbuf", [128, 256], F), "T3": ("sbuf", [128, 16, 8], F), "CC": ("sbuf", [128, NC], B),
-    "PI": ("sbuf", [128, 4], I), "PJ": ("sbuf", [128, 4], I), "CF": ("sbuf", [128, 24], F),
+    "IF": ("sbuf", [128, 128], F), "PF": ("sbuf", [128, 128], F),
+    "YI": ("sbuf", [128, 256], B), "T3": ("sbuf", [128, 8, 8], F), "CC": ("sbuf", [128, NC], B),
+    "PI": ("sbuf", [128, 4], I), "PJ": ("sbuf", [128, 5], I), "CF": ("sbuf", [128, 24], F),
     "CI": ("sbuf", [128, 64], I), "VI": ("sbuf", [128, 64], I),
     "LP": ("sbuf", [128, 328], I), "LB": ("sbuf", [128, 256], I),
     "ON": ("sbuf", [128, NT * 328], U16), "OC": ("sbuf", [128, 256], U16), "DD": ("sbuf", [128, 3, 256], B),
-    "MI": ("sbuf", [128, 128], I), "OB": ("sbuf", [128, 4], F), "TH": ("sbuf", [128, 4], F),
+    "MI": ("sbuf", [128, 256], I), "OB": ("sbuf", [128, 4], F), "TH": ("sbuf", [128, 4], F),
     "CB": ("sbuf", [128, NT * 16], F),
     "ST": ("sbuf", [128, 4, 128], F), "SHI": ("sbuf", [128, 4, 128], B), "SLO": ("sbuf", [128, 4, 128], B),
     "OA": ("sbuf", [128, 256], U16), "MN": ("sbuf", [128, 64], F), "M2": ("sbuf", [128, 128], F), "RL": ("sbuf", [128, 256], B),
@@ -31,34 +31,35 @@ SCRATCH = {
     "K0": ("psum", [128, 512], F), "K1": ("psum", [128, 512], F), "K2": ("psum", [128, 512], F), "K3": ("psum", [128, 512], F),
     "N0": ("psum", [128, 512], F), "N1": ("psum", [128, 512], F), "R0": ("psum", [128, 512], F), "R1": ("psum", [128, 512], F),
 }
-SEMAPHORES = (["cV", "cS", "cP", "cG", "locA", "locH0", "locH1", "dM", "dSN", "dHR", "dL", "dH", "dO", "dT", "dR", "dOwn", "dOH", "dOut"]
+SEMAPHORES = (["cV", "cS", "cP", "cG", "locA", "locH0", "locH1", "locH2", "dM", "dSN", "dHR", "dL", "dH", "dO", "dT", "dR", "dOwn", "dOH", "dOut"]
               + ["dW%d" % t for t in range(NT)] + ["arrA%d" % t for t in range(NT)] + ["arrH%d" % t for t in range(NT)])
 
 MAIN0 = {
-    "V": "x0 x2 c01 x4 w0 c23 x6 c45 w4 c67 m1 p0 m2 p1 r0 r1 r2 r3 p2 l1 p3 p4 g1 p5 g2 p6 g3 p7 o0 g5 b1 i6 i7 j7 b2",
-    "S": "x1 x3 x5 x7 w1 m0 w2 w3 w5 w6 w7 l0 a0 a1 a2 a3 g0 a4 a5 g4 b0 a6 a7 j6",
-    "P": "A01 A23 M0 M1 A45 A67 M2 M3 K0 K1 K2 K3 X0 E0 E1 E2 E3 Z0 C0 C1 C2 C3 C4",
+    "V": "x0 x2 y1 c01 x4 c23 w0 x6 c45 y0 w4 c67 p0 m1 p1 m2 p2 r0 r1 r2 r3 l1 p3 p4 g1 p5 g2 p6 g3 p7 g5 b1 i6 i7 j7 b2",
+    "S": "x1 x3 x5 x7 w1 w2 m0 w3 w5 w6 w7 l0 a01 a2 g0 a3 a4 a5 g4 b0 a6 a7 j6",
+    "P": "A01 A23 M0 M1 A45 A67 M2 M3 K0 K1 K2 K3 X0 E0 E1 E2 E3 Z0 C0 C1 C2 C3 F0 F2 F1 F3",
     "G": "L0",
 }
 MAIN = {
-    "V": "x0 x1 c0 x2 c1 x3 c2 x4 c3 x5 c4 x6 c5 x7 c6 p0 c7 p1 m1 m2 p2 r0 r1 r2 r3 p3 p4 l1 p5 g1 p6 g3 p7 g4 g5 b1 i6 i7 j7 b2",
-    "S": "w0 w1 w2 w3 w4 w5 m0 w6 a0 w7 a1 l0 g0 a2 a3 g2 a4 a5 b0 a6 a7 j6",
-    "P": "A0 A1 A2 A3 M0 A4 A5 M1 A6 A7 M2 M3 K0 K1 K2 K3 E0 E1 E2 E3 C0 C1 Z0 C2 C3 C4",
+    "V": "x0 x1 c0 x2 c1 x3 c2 x4 c3 x5 c4 x6 c5 x7 c6 p0 c7 p1 m1 m2 p23 r0 r1 r2 r3 p45 l1 g1 p6 g3 p7 g4 g5 b1 i6 i7 j7 b2",
+    "S": "w0 w1 w2 w3 w4 w5 m0 w6 a0 w7 a1 l0 g0 a23 g2 a45 b0 a6 a7 j6",
+    "P": "A0 A1 A2 A3 M0 A4 A5 M1 A6 A7 M2 M3 K0 K1 K2 K3 E0 E1 E2 E3 C0 C1 Z0 C2 C3 F0 F1 F2 F3",
     "G": "L0",
 }
 TAIL = {
-    "V": "n0 n1 n2 n4 n3 n5 n6 v0 u0 b3 n7 n8 u1 n9 h0 h1 u2 u3 h2 h3 s0",
-    "S": "e0 e1 e2 e3 s1 s2 s3",
-    "P": "C5 Y0 C6",
-    "G": "t0 t1 t2 k03",
+    "V": "n0 n1 n2 n4 n3 n5 n6 v0 u0 b3 n7 n8 u1 n9 h01 u2 d3 h2 d4 o0",
+    "S": "e0 e1 e2 d0 e3 d2 s0 s1 s2",
+    "P": "D2 Y0 D3 d1 X1",
+    "G": "v1 t0 t1 t2 t3 k03",
 }
 LAST = {
     "V": "n0 n4 n2 n5 n1 n6 f0 b3 n7 u0 n8 n9 h0 u1 h1 u2 h2 u3 h3",
-    "S": "e0 e1 e2 e3 f2",
-    "P": "C5 C6 f1",
+    "S": "e0 e1 e2 e3 f2 f3",
+    "P": "D2 D3 f1",
     "G": "k0 k1 k2 k3",
 }
-CH_STEP = (0, 8, 28, 50, 64)
+CH_STEP = (0, 10, 26, 38, 64)
+OUTQ = "S"
 CH_LAST = (0, 12, 32, 54, 64)
 
 
@@ -150,7 +151,8 @@ def rank_program(g, core, T, topo):
         eng[d] = [x for x in topo.engines(core, peers[d]) if x not in far_eng]
     arrive = sum(len(v) for v in eng.values())
 
-    alone = {d: topo.engines(core, peers[d]) for d in near}
+    alone = {d: topo.engines(core, peers[d]) for d in peers}
+    halves = [{d: eng[d] if d in far else eng[d][j * len(eng[d]) // 2:(j + 1) * len(eng[d]) // 2] for d in peers} for j in range(2)]
 
     def send(src, dst, ds, rsem, lsem, keys, eng=eng):
         wait("G", deps("G", keys, (), ()))
@@ -172,106 +174,104 @@ def rank_program(g, core, T, topo):
     HW, AC = [T.HW0, T.HW1], [T.AC0, T.AC1]
     K, N, R = [T.K0, T.K1, T.K2, T.K3], [T.N0, T.N1], [T.R0, T.R1]
     CF = T.CF
-    c_p, c_pm, c_r, c_r4, c_g, c_x, c_4, c_l0, c_m0, c_l1, c_m1, c_rr, c_t, c_ev = [CF[:, j:j + 1] for j in range(14)]
+    c_p, c_pm, c_r, c_r4, c_q, c_g, c_x, c_4, c_l0, c_m0, c_l1, c_m1, c_rr, c_t, c_ev = [CF[:, j:j + 1] for j in range(15)]
     OH, RH = 16, 20
 
     IB, W2 = T.IW[:, 0:128], [T.W0, T.W1]
-    dma("S", "dM", [(T.MI[:, 0:64], T.mt[:]), (T.MI[:, 64:128], T.mm[:])], w=["MI"])
+    dma("S", "dM", [(T.MI[0:64, 0:128], T.mt[:]), (T.MI[64:128, 0:128], T.mt[:]), (T.MI[0:64, 128:256], T.mm[:])], w=["MI"])
     dma("Y", "dSN", moved(T.LP, 256, T.sn, 0, 72, 7), w=["SN"])
     dma("Y", "dHR", moved(T.HR, 0, T.h0, 0, NV, 7), w=["HR0", "HR1", "HR2", "HR3"])
     wait("Y", [lastw["HR0"]])
     dma("Y", "dL", [(T.LP[:, 0:256], T.pd[:]), (T.LB[:], T.lb[:]), (T.OB[:], T.obs[:])], w=["PD", "LB", "OB"])
-    dma("Y", "dH", [(T.HW0[:, 0:NV], T.h0[:])], w=["HW0o0", "HW0o1", "HW0o2", "HW0o3"])
     dma("Y", "dW0", [(T.W0[:, 0:NA], T.wv[:])], w=["Wa"])
-    op("G", lambda: g.iota(T.PI[:], [[112, 4]], 0, 1), w=["PI"])
+    op("G", lambda: g.iota(T.PI[:], [[56, 4]], 0, 1), w=["PI"])
     op("G", lambda: g.iota(T.YI[:], [[0, 2], [1, 128]], 0, 0, allow_small_or_imprecise_dtypes=True), w=["YI"])
     op("G", lambda: g.iota(T.CC[:], [[1, 64], [64, 4]], 0, 0, allow_small_or_imprecise_dtypes=True), w=["CC"])
-    op("G", lambda: g.iota(T.T3[:], [[1, 16], [16, 8]], 0, 0, allow_small_or_imprecise_dtypes=True), w=["T3"])
+    op("G", lambda: g.iota(T.T3[:], [[1, 8], [8, 8]], 0, 0, allow_small_or_imprecise_dtypes=True), w=["T3"])
     op("G", lambda: g.iota(T.CI[:], [[16, 64]], 0, 0), w=["CI"])
     dma("G", "dT", [(T.TH[:, 0:1], T.th[:])], w=["TH"], slow=True)
     op("V", lambda: g.vector.memset(T.UM[:], 0.0), w=["UM"])
-    op("V", [ts(T.PJ[:, 0:2], T.PI[:, 0:2], 127, A.bitwise_and), ts(T.PJ[:, 2:3], T.PI[:, 0:1], 15, A.bitwise_and),
-             ts(T.PJ[:, 3:4], T.PI[:, 0:1], 3, A.bitwise_and)], r=["PI"], w=["PJ"])
-    op("V", cp(CF[:, 0:4], T.PJ[:]), r=["PJ"], w=["CF"])
+    op("V", [ts(T.PJ[:, 0:2], T.PI[:, 0:4:2], 127, A.bitwise_and), ts(T.PJ[:, 2:3], T.PI[:, 0:1], 15, A.bitwise_and),
+             ts(T.PJ[:, 3:4], T.PI[:, 0:1], 3, A.bitwise_and), ts(T.PJ[:, 4:5], T.PI[:, 1:2], 63, A.bitwise_and)], r=["PI"], w=["PJ"])
+    op("V", cp(CF[:, 0:5], T.PJ[:]), r=["PJ"], w=["CF"])
     op("V", [ts(c_4, c_r, 4.0, A.is_ge), ts(c_x, c_r, 3.0, A.is_equal)], r=["CF"], w=["c_4"])
     op("V", ts(T.IW[:], T.YI[:], c_p, A.is_equal), r=["YI", "CF"], w=["IB"])
     op("V", ts(CF[:, OH:OH + 4], T.YI[:, 0:4], c_r4, A.is_equal, c_4, A.mult), r=["YI", "c_4"], w=["OH"])
-    op("V", ts(T.UM[:, :, 3:131:16], T.T3[:], c_pm, A.is_equal), r=["T3", "CF"], w=["UM"])
+    op("V", [ts(T.I14[:], IB, 16384.0, A.mult), ts(T.ZB[:], IB, 0.0, A.mult), cp(T.IF[:], IB)], r=["IB"], w=["I14", "ZB", "IF"])
+    op("V", [ts(T.UM[64 * j:64 * j + 64, :, 3 + j:131:16], T.T3[64 * j:64 * j + 64], CF[64 * j:64 * j + 64, 4:5], A.is_equal) for j in range(2)],
+       r=["T3", "CF"], w=["UM"])
     op("V", [ts(T.SX[:, j:NV:4], T.CC[:], c_x, A.mult, CF[:, OH + j:OH + j + 1], A.add) for j in range(4)], r=["CC", "OH"], w=["SX"])
     for b in range(2):
         op("P", mm(N[b][:], IB, T.SX[:, 512 * b:512 * b + 512], True, False), r=["IB", "SX"], w=["N%d" % b], bk=["N%d" % b])
 
-    def U(i, row):
-        return T.UM[:, i, 3 - row:131 - row]
-
     pcs = [T.PC[:, 64 * j:64 * j + 64] for j in range(4)]
+    op("V", cp(T.PC[:, 0:128], T.MI[:, 0:128]), r=["MI"], w=["PC0"])
+    op("V", ts(T.TI[0:64, :], T.MI[0:64, 128:256], 511, A.bitwise_and), r=["MI"], w=["TIa"])
+    op("V", tt(T.PC[64:128, 0:128], T.MI[64:128, 0:128], T.PC[64:128, 0:128], A.subtract), r=["MI", "PC0"], w=["PC1"])
+    op("V", ts(T.PC[0:64, 128:256], T.TI[0:64, :], -256.0, A.add), r=["TIa"], w=["PC3"])
     op("V", cp(T.ON[:, 256:328], T.LP[:, 256:328]), r=["SN"], w=["ONs"])
-    op("V", cp(pcs[0], T.MI[:, 0:64]), r=["MI"], w=["PC0"])
-    op("V", ts(T.TI[:, 0:64], T.MI[:, 64:128], 511, A.bitwise_and), r=["MI"], w=["TIa"])
-    op("V", tt(pcs[1], T.MI[:, 0:64], pcs[0], A.subtract), r=["MI", "PC0"], w=["PC1"])
-    op("V", ts(pcs[3], T.TI[:, 0:64], -256.0, A.add), r=["TIa"], w=["PC3"])
 
     hr_keys = ["HR0", "HR1", "HR2", "HR3"]
 
     def show(e, j, t=0):
-        c0, c1 = (24 * (far[j] - 1), 24 * far[j]) if j < 2 else (24 * near[0] - 48 + 12 * j, 24 * near[0] - 36 + 12 * j)
-        o = 328 * t + 256
-        op(e, copy(e, T.SH[:, 16 * c0:16 * c1], T.HR[:, 0:NV].indirect(T.ON[:, o + c0:o + c1])), r=hr_keys + ["ONr" if t else "ONs"], w=["SH%d" % j])
+        c0 = 24 * ((far + near)[j] - 1)
+        o = 328 * t + 256 + c0
+        op(e, copy(e, T.SH[:, 16 * c0:16 * c0 + NS], T.HR[:, 0:NV].indirect(T.ON[:, o:o + 24])), r=hr_keys + ["ONr" if t else "ONs"], w=["SH%d" % j])
 
-    def send_h(t, j):
-        keys = ["SH%d" % (2 * j), "SH%d" % (2 * j + 1)]
-        send(block(T.SH), block(HW[t % 2], NV), [far, near][j], "arrH%d" % t, "locH%d" % j, keys, alone if t == 0 and j else eng)
-        for k in keys:
-            readers.setdefault(k, []).append(("locH%d" % j, cnt["locH%d" % j]))
-        lastw["HW%dr" % (t % 2)] = ("arrH%d" % t, arrive + (0 if t else sum(len(alone[d]) - len(eng[d]) for d in near)))
+    def send_h(t, js):
+        use = {d: alone[d] if d in far else eng[d] if t else halves[0][d] for d in peers}
+        loc = "locH%d" % js[0]
+        send(block(T.SH), block(HW[t % 2], NV), [(far + near)[j] for j in js], "arrH%d" % t, loc, ["SH%d" % j for j in js], use)
+        for j in js:
+            readers.setdefault("SH%d" % j, []).append((loc, cnt[loc]))
+        lastw["HW%dr" % (t % 2)] = ("arrH%d" % t, sum(len(v) for v in use.values()))
 
     show("S", 2)
-    show("V", 3)
-    send_h(0, 1)
+    send_h(0, [2])
     for b in range(2):
         fns = []
-        for i in range(8 * b, 8 * b + 8):
-            o = N[b][:, 64 * (i % 8):64 * (i % 8) + 64]
-            fns += [mm(o, U(i, 0), pcs[0], False, False), mm(o, U(i, 1), pcs[1], False, False), mm(o, U(i, 2), pcs[3], False, i % 8 == 7)]
+        for i in range(4 * b, 4 * b + 4):
+            o = N[b][:, 128 * (i % 4):128 * (i % 4) + 128]
+            fns += [mm(o, T.UM[:, i, 3:131], T.PC[:, 0:128], False, False), mm(o, T.UM[0:64, i, 1:129], T.PC[0:64, 128:256], False, i % 4 == 3)]
         op("P", fns, r=["UM", "PC0", "PC1", "PC3"], w=["N%d" % b], bk=["N%d" % b])
     op("V", [ts(c_g, c_p, c_r, A.subtract, 15.0, A.add), ts(c_l0, c_r, 2.0, A.is_equal, 4.0, A.mult), ts(c_m0, c_r, 2.0, A.is_lt),
              ts(c_l1, c_r, 12.0, A.is_ge, 4.0, A.mult), ts(c_m1, c_r, 12.0, A.is_lt, c_4, A.mult), ts(c_rr, c_r, c_r4, A.subtract)],
        r=["CF", "c_4"], w=["c_g"])
     for b in range(2):
-        op("SV"[b], copy("SV"[b], T.SW[:, 512 * b:512 * b + 512], N[b][:]), r=["N%d" % b], w=["SW%d" % b], bk=["N%d" % b])
+        op("V", cp(T.SW[:, 512 * b:512 * b + 512], N[b][:]), r=["N%d" % b], w=["SW%d" % b], bk=["N%d" % b])
     for b in range(2):
         op("P", mm(K[b][:], T.IW[:, 112:240], T.SW[:, 512 * b:512 * b + 512], True, True), r=["SW%d" % b], w=["KA%d" % b], bk=["K%d" % b])
     for b in range(2):
         op("SV"[b], copy("SV"[b], T.SA[:, 576 * b:576 * b + 576], T.SW[:, 0:NV].indirect(T.ON[:, 256 + 36 * b:292 + 36 * b])),
            r=["SW0", "SW1", "ONs"], w=["SA%d" % b])
-    send(block(T.SA), block(T.AX, NV), far + near, "arrA0", "locA", ["SA0", "SA1"])
-    lastw["AXr0"] = ("arrA0", arrive)
-    show("S", 0)
-    show("V", 1)
-    send_h(0, 0)
+    send(block(T.SA), block(T.AX, NV), far + near, "arrA0", "locA", ["SA0", "SA1"], halves[1])
+    lastw["AXr0"] = ("arrA0", sum(len(v) for v in halves[1].values()))
+    dma("Y", "dH", [(T.HW0[:, 0:NV], T.h0[:])], r=["AXr0"], w=["HW0o0", "HW0o1", "HW0o2", "HW0o3"])
+    for j in range(2):
+        show("S", j)
+        send_h(0, [j])
     op("S", [act(T.AX[:, 512 * b:512 * b + 512], K[b][:], AF.Copy) for b in range(2)], r=["KA0", "KA1"], w=["AXo0"], bk=["K0", "K1"])
 
+    op("V", [ts(c_t, c_pm, c_r, A.subtract, c_r4, A.add), ts(CF[:, RH:RH + 4], T.YI[:, 0:16:4], c_rr, A.is_equal),
+             ts(c_ev, c_rr, 8.0, A.is_equal, -192.0, A.mult), ts(T.VI[:], T.CI[:], c_r, A.add)], r=["c_g", "CI"], w=["c_t", "VI"])
+    op("V", [ts(w[:], T.YI[:, 0:w.shape[1]], c_g, A.is_equal, c, A.mult)
+             for w, c in ((T.WL0, c_l0), (T.WM0, c_m0), (T.WL1, c_l1), (T.WM1, c_m1), (T.WX, c_x), (T.WC, 16384.0))], r=["YI", "c_g"], w=["WW"])
+    op("V", ts(c_t, c_t, 12.0, A.add), r=["c_t"], w=["c_t"])
+    op("V", [f for k in range(4) for f in (ts(T.ST[:, k, 0:64], T.LB[:, 64 * k:64 * k + 64], 1024.0 + 4096 * k, A.add),
+                                           ts(T.ST[:, k, 64:128], T.LP[:, 64 * k:64 * k + 64], 4096.0 * k, A.add))], r=["LB", "PD"], w=["ST"])
+    op("S", act(T.SHI[:], T.ST[:], AF.Copy), r=["ST"], w=["SHI"])
     op("V", cp(T.ON[:, 0:256], T.LP[:, 0:256]), r=["PD"], w=["ONp"])
-    for w, c in ((T.WL0, c_l0), (T.WM0, c_m0), (T.WL1, c_l1), (T.WM1, c_m1), (T.WX, c_x), (T.WC, 16384.0)):
-        op("V", ts(w[:], T.YI[:, 0:w.shape[1]], c_g, A.is_equal, c, A.mult), r=["YI", "c_g"], w=["WW"])
-    for k in range(4):
-        op("V", [ts(T.ST[:, k, 0:64], T.LB[:, 64 * k:64 * k + 64], 1024.0 + 4096 * k, A.add),
-                 ts(T.ST[:, k, 64:128], T.LP[:, 64 * k:64 * k + 64], 4096.0 * k, A.add)], r=["LB", "PD"], w=["ST%d" % k])
-    stk = ["ST%d" % k for k in range(4)]
-    op("S", act(T.SHI[:], T.ST[:], AF.Copy), r=stk, w=["SHI"])
-    op("V", [ts(T.DD[:, j, :], T.LP[:, 0:256], float(NV + NS * j), A.is_ge, float(NC), A.mult) for j in range(3)], r=["PD"], w=["DD"])
-    op("V", [ts(c_t, c_pm, c_rr, A.subtract, c_r4, A.subtract), ts(CF[:, RH:RH + 4], T.YI[:, 0:16:4], c_rr, A.is_equal),
-             ts(c_ev, c_rr, 8.0, A.is_equal, -192.0, A.mult)], r=["c_g"], w=["c_t"])
-    op("V", tt(T.SLO[:], T.ST[:], T.SHI[:], A.subtract), r=stk + ["SHI"], w=["SLO"])
-    op("V", ts(c_t, c_t, c_r4, A.add, 12.0, A.add), r=["c_t"], w=["c_t"])
-    op("V", ts(T.VI[:], T.CI[:], c_r, A.add), r=["CI", "CF"], w=["VI"])
-    op("V", [ts(T.CM[:, j, :], T.YI[:, 0:168], c_t, A.is_equal, CF[:, RH + j:RH + j + 1], A.mult) for j in range(4)], r=["c_t"], w=["CM"])
+    op("V", tt(T.SLO[:], T.ST[:], T.SHI[:], A.subtract), r=["ST", "SHI"], w=["SLO"])
     op("S", [act(T.CB[:, 0:4], T.OB[:], AF.Copy), act(T.CB[:, 4:8], T.OB[:], AF.Copy, scale=0.125),
              act(T.CB[:, 8:9], T.TH[:, 0:1], AF.Copy), act(T.CB[:, 9:10], T.TH[:, 0:1], AF.Copy, scale=-1.0)], r=["OB", "TH"], w=["CB"])
-    op("S", act(T.I14[:], IB, AF.Copy, scale=16384.0), r=["IB"], w=["I14"])
-    op("S", act(T.ZB[:], IB, AF.Copy, scale=0.0), r=["IB"], w=["ZB"])
-    op("S", act(T.W0[:, NA:2 * NA], T.W0[:, 0:NA], AF.Copy), r=["Wa"], w=["W0"])
-    op("S", act(T.IF[:], IB, AF.Copy), r=["IB"], w=["IF"])
+    op("S", act(T.W0[:, NA:NA + 768], T.W0[:, 0:768], AF.Copy), r=["Wa"], w=["Wb"])
+    op("V", cp(T.W0[:, NA + 768:2 * NA], T.W0[:, 768:NA]), r=["Wa"], w=["W0"])
+
+    def later(e, j):
+        if j == 0:
+            op("V", [ts(T.DD[:, i, :], T.ON[:, 0:256], float(NV + NS * i), A.is_ge, float(NC), A.mult) for i in range(3)], r=["ONp"], w=["DD"])
+        else:
+            op("V", [ts(T.CM[:, i, :], T.YI[:, 0:168], c_t, A.is_equal, CF[:, RH + i:RH + i + 1], A.mult) for i in range(4)], r=["c_t"], w=["CM"])
 
     def shifted(w, c0, t=0):
         c = (c0 - 16 * t) % 128
@@ -280,6 +280,7 @@ def rank_program(g, core, T, topo):
     def wrap(out, w, src, k, last, first=False, t=0):
         return [mm(out, shifted(w, 15 - i, t), src[:, 1024 * k + i:1024 * k + 1024:16], first and i == 0, last and i == 15) for i in range(16)]
 
+    UP = ("K2", "K2", "K3", "N1")
     turn = {}
 
     def bank_a(js, new=False):
@@ -343,16 +344,19 @@ def rank_program(g, core, T, topo):
                r=["IB", "SHI", "SLO", "WW"] + two(ag, k), w=["KA%d" % k, "KB%d" % k], bk=["K%d" % k])
 
         def xwrap(e, j):
-            fns = [mm(R[1][:, 256:512], IB, T.DD[:, i, :], i == 0, False) for i in range(3)]
-            for k in range(4):
-                fns += wrap(R[1][:, 256 + 64 * k:320 + 64 * k], T.WX, T.MK, k, k == 3)
-            op("P", fns, r=["IB", "DD", "WW"] + names("MK", range(8)), w=["PX"], bk=["R1"])
+            if t == 0:
+                c0 = 256 + 128 * j
+                fns = [mm(R[1][:, c0:c0 + 128], IB, T.DD[:, i, 128 * j:128 * j + 128], i == 0, False) for i in range(3)]
+                for k in range(2):
+                    fns += wrap(R[1][:, c0 + 64 * k:c0 + 64 * k + 64], T.WX, T.MK, 2 * j + k, k == 1)
+                op("P", fns, r=["IB", "DD", "WW"] + names("MK", range(8)), w=["PX"], bk=["R1"])
 
         def xconv(e, j):
-            op("V", cp(T.OC[:], R[1][:, 256:512]), r=["PX"], w=["OC"], bk=["R1"])
+            if t == 0:
+                op("V", cp(T.OC[:], R[1][:, 256:512]), r=["PX"], w=["OC"], bk=["R1"])
 
         def wa(e, js):
-            op(e, copy(e, sl(T.WA, js), W2[p][:, 0:4096].indirect(sl(T.OA, js, 32))), r=["W%d" % p] + names("OA", js), w=names("WA", js))
+            op(e, copy(e, sl(T.WA, js), W2[p][:, 0:4096].indirect(sl(T.OA, js, 32))), r=["W%d" % p, "Wb"] + names("OA", js), w=names("WA", js))
 
         def loads(e, j):
             wait("Y", [lastw["PR0"]])
@@ -404,16 +408,22 @@ def rank_program(g, core, T, topo):
 
         def evac(e, j):
             o, i = T.SC[:], N[0][:, 0:NC]
-            op(e, ts(o, i, c_ev, A.add) if e == "V" else act(o, i, AF.Identity, bias=c_ev), r=["N0", "c_t"], w=["SC"], bk=["N0"])
-            dma("Y", "dOwn", moved(AC[q], 0, T.SC, 0, NC), r=["SC"], w=["AXo%d" % (t + 1)])
-
-        def sends(e, j):
             if j == 0:
+                op(e, ts(o, i, c_ev, A.add) if e == "V" else act(o, i, AF.Identity, bias=c_ev), r=["N0", "c_t"], w=["SC"], bk=["N0"])
+            elif j == 1:
+                dma("Y", "dOwn", moved(AC[q], 0, T.SC, 0, NC), r=["SC"], w=["AXo%d" % (t + 1)])
+            elif j == 2:
+                op("P", mm(N[1][:, 0:NC], T.IW[:, 112:240], o, True, True), r=["SC"], w=["KM2", "KM3"], bk=["N1"])
+            else:
+                op(e, copy(e, AC[q][:, 0:NC], N[1][:, 0:NC]), r=["KM2"], w=["AXo%d" % (t + 1)], bk=["N1"])
+
+        def sends(e, js):
+            if js[0] == 0:
                 send(lambda d: T.SC[:], lambda d: AC[q][:, NC * d:NC * d + NC], far + near, "arrA%d" % (t + 1), "locA", ["SC"])
                 readers["SC"].append(("locA", cnt["locA"]))
                 lastw["AXr%d" % (t + 1)] = ("arrA%d" % (t + 1), arrive)
             else:
-                send_h(t + 1, j - 1)
+                send_h(t + 1, [j - 1 for j in js])
 
         def prod(e, js):
             op("V", tt(sl(T.PR, js), HW[p][:, 0:NW].indirect(T.ON[:, 328 * t + 32 * js[0]:328 * t + 32 * js[-1] + 32]), sl(T.WA, js), A.mult),
@@ -441,12 +451,18 @@ def rank_program(g, core, T, topo):
             if k < 2:
                 for which, o in (("A", K[k][:, 0:64]), ("B", ps_b(k))):
                     op("P", wrap(o, T.WC, T.FL, k, which == "B"), r=["WW"] + two("FL", k), w=["K%s%d" % (which, k)], bk=["K%d" % k])
-            elif k == 2:
-                op("P", wrap(K[2][:, 0:64], T.WC, T.FL, 2, True), r=["WW"] + two("FL", 2), w=["KA2"], bk=["K2"])
-            elif k < 5:
-                op("P", wrap(K[3][:, 0:64], T.WC, T.FL, 3, True)[k - 3::2], r=["WW", "F%d6" % (k - 3), "F%d7" % (k - 3)], w=["KA3"], bk=["K3"])
             else:
-                op("P", wrap(ps_b(k - 3), T.WC, T.FL, k - 3, k == 6), w=["KB%d" % (k - 3)], bk=["R0"])
+                op("P", eighth(k + 2, range(16), k == 3), r=["WW", "FL%d" % (k + 2)], w=["KA2"], bk=["K2"])
+
+        def eighth(j, rows, stop):
+            o = K[j // 2][:, 32 * (j % 2):32 * (j % 2) + 32]
+            return [mm(o, shifted(T.WC, 15 - i), T.FL[:, 512 * j + i:512 * j + 512:16], False, stop and i == 15) for i in rows]
+
+        def ends(e, j):
+            op("P", eighth(6 + j // 2, range(j % 2, 16, 2), j == 3), r=["WW", "F%d%d" % (j % 2, 6 + j // 2)], w=["KA3"], bk=["K3"])
+
+        def second(e, k):
+            op("P", wrap(ps_b(k), T.WC, T.FL, k, k == 3), r=two("FL", 2) if k == 2 else ["F06", "F16", "F07", "F17"], w=["KB%d" % k], bk=["R0"])
 
         def best(e, k):
             o, src, bank = [(T.BE[:], K[0][:, 0:128], "K0"), (T.BE[:], K[1][:, 0:128], "K1"),
@@ -488,6 +504,27 @@ def rank_program(g, core, T, topo):
         def hn(e, js):
             op("V", tt(c4(T.HR, js), HW[p][:, 0:NW].indirect(o4(64, js)), c4(T.UU, js), A.add), r=hwk + ["OSb"] + names("UU", js), w=names("HR", js))
 
+        def dense(e, j):
+            js, n = [3], 16 * (CH[4] - CH[3])
+            if j == 0:
+                op("S", act(T.SW[:, 0:n], T.WA[:, 0:4096].indirect(o4(0, js)), AF.Copy), r=names("WA", range(8)) + ["OSa"], w=["SW0"])
+            elif j == 1:
+                op("P", mm(K[0][:, 0:n], IB, T.SW[:, 0:n], True, True), r=["SW0"], w=["KA0", "KB0"], bk=["K0"])
+            elif j == 2:
+                op("S", act(c4(T.UU, js), HW[p][:, 0:NW].indirect(o4(64, js)), AF.Copy), r=hwk + ["OSb"], w=["UU3"])
+            elif j == 3:
+                op("V", tt(K[1][:, 0:n], c4(T.ES, js), K[0][:, 0:n], A.mult), r=["ES3", "KA0"], w=["KA1", "KB1"], bk=["K0", "K1"])
+            else:
+                op("V", tt(c4(T.HR, js), c4(T.UU, js), K[1][:, 0:n], A.add), r=["UU3", "KA1"], w=["HR3"], bk=["K1"])
+
+        def shift(e, js):
+            b = UP[js[-1]]
+            op("P", mm(T[b][:, 0:16 * (CH[js[-1] + 1] - CH[js[0]])], T.PF[:], c4(T.HR, js), True, True), r=["PF"] + names("HR", js), w=["UP" + b], bk=[b])
+
+        def own(e, js):
+            b = UP[js[-1]]
+            op(e, copy(e, c4(HW[q], js), T[b][:, 0:16 * (CH[js[-1] + 1] - CH[js[0]])]), r=["UP" + b], w=names("HW%do" % q, js), bk=[b])
+
         def keep(e, js):
             c0, n = 16 * CH[js[0]], 16 * (CH[js[-1] + 1] - CH[js[0]])
             if last:
@@ -503,28 +540,34 @@ def rank_program(g, core, T, topo):
             elif j == 1:
                 op("P", [(lambda i=i: g.tensor.transpose(N[0][0:32, 128 * i:128 * i + 128], T.FO[:, i:128:4], T.IF[:])) for i in range(4)],
                    r=["FO", "IF"], w=["N0"], bk=["N0"])
-            else:
+            elif j == 2:
                 op("S", [act(T.FT[:, :, i, :], N[0][0:32, 128 * i:128 * i + 128], AF.Copy) for i in range(4)], r=["N0"], w=["FT"], bk=["N0"])
-                dma("S", "dOut", [(T.ymt[gg, :], T.FT[0:16, (gg + t) % 8]) for gg in range(8)]
+            else:
+                dma(OUTQ, "dOut", [(T.ymt[gg, :], T.FT[0:16, (gg + t) % 8]) for gg in range(8)]
                     + [(T.ymm[gg, :], T.FT[16:32, (gg + t) % 8]) for gg in range(8)], r=["FT"])
 
         return {"x": aux, "w": wa, "p": prod, "a": absd, "g": gt, "A": mwrap, "c": conv, "M": Mwrap, "K": keys, "r": rel, "E": addrel,
                 "i": lambda e, j: half(e, j, 0), "j": lambda e, j: half(e, j, 1),
-                "C": counts, "b": best, "m": least, "l": split, "Z": early, "Y": late, "v": evac, "n": survivors, "X": xwrap, "o": xconv,
-                "e": es, "u": uu, "h": hn, "k": keep, "s": lambda e, j: show(e, j, t + 1), "t": sends, "f": final,
+                "C": counts, "F": ends, "D": second, "b": best, "m": least, "l": split, "Z": early, "Y": late, "v": evac, "n": survivors, "X": xwrap, "o": xconv, "y": later,
+                "e": es, "u": uu, "h": hn, "k": keep, "d": dense, "R": shift, "q": own, "s": lambda e, j: show(e, j, t + 1), "t": sends, "f": final,
                 "L": loads if not last else lambda e, j: None}
 
     def needs(kind, j):
         two = lambda k: names(k, (2 * j, 2 * j + 1))
-        return {"x": ["-t0", "-o0"], "A": ["x%d" % j], "M": two("x") + ["-v0"], "K": two("x") + ["-n0", "-n7"], "L": ["p0"], "c": ["A%d" % j],
-                "w": ["c%d" % j, "-u3"], "m": [["M0", "M1"], ["m0", "M2", "M3"], ["m1"]][min(j, 2)], "r": ["m2"],
+        return {"x": ["-t0", "-o0", "-v1", "-v3"], "A": ["x%d" % j], "M": two("x") + ["-v0"] + names("-q", range(4)) * (j >= 2),
+                "K": two("x") + ["-n0", "-n7", "-d4"] + names("-q", range(4)), "L": ["p0"], "c": ["A%d" % j],
+                "w": ["c%d" % j, "-u2", "-u3", "-d0"], "m": [["M0", "M1"], ["m0", "M2", "M3"], ["m1"]][min(j, 2)], "r": ["m2"],
                 "l": ["m2"] if j == 0 else ["l0"], "E": ["r%d" % j, "K%d" % j] + (names("c", range(8)) if j == 2 else ["E2"] if j == 3 else []),
-                "i": ["a%d" % j], "j": ["a%d" % j], "Z": ["l1", "r0", "r1"], "p": ["w%d" % j, "-t1", "-t2", "-e3", "-k3"], "a": ["p%d" % j], "g": ["a%d" % j],
-                "C": two("g") + ["E%d" % j] if j < 3 else ["E3", "i6", "i7"] if j == 3 else ["C%d" % (j - 1), "j6", "j7"],
-                "b": [["C0"], ["C1", "b0"], ["C2", "b1"], ["C6", "b1"]][min(j, 3)], "X": names("x", range(8)) + names("c", range(8)), "o": ["X0"],
-                "n": ["b2", "C4"] if j == 0 else ["b3"] if j == 7 else ["n%d" % {2: 0, 3: 1, 4: 0}.get(j, j - 1)],
-                "Y": ["n2", "n3", "Z0"], "v": ["Y0"], "e": ["n6"], "u": ["e%d" % j], "h": ["u%d" % j, "n9"], "k": ["h%d" % j], "s": names("h", range(4)) + ["L0"],
-                "t": [["v0"], ["s0", "s1"], ["s2", "s3"]][min(j, 2)], "f": ["n1", "n2"] if j == 0 else ["f%d" % (j - 1)]}[kind]
+                "i": ["a%d" % j], "j": ["a%d" % j], "Z": ["l1", "r0", "r1", "y1"], "p": ["w%d" % j, "-t1", "-t2", "-t3", "-e3"] + names("-k", range(4)) + names("-q", range(4)), "a": ["p%d" % j], "g": ["a%d" % j],
+                "C": two("g") + ["E%d" % j] if j < 2 else ["E2", "g%d" % (j + 2)] + ["C2"] * (j == 3),
+                "F": ["E3", "%s%d" % ("ij"[j % 2], 6 + j // 2)] + names("F", range(3)) * (j == 3),
+                "D": ["E3", "g4", "g5"] + ["D2", "F3"] * (j == 3),
+                "b": [["C0"], ["C1", "b0"], ["C3", "b1"], ["D3", "b1"]][min(j, 3)], "X": names("x", range(8)) + names("c", range(8)) + ["y0"], "o": ["X0", "X1"], "y": [],
+                "n": ["b2", "F3"] if j == 0 else ["b3"] if j == 7 else ["n%d" % {2: 0, 3: 1, 4: 0}.get(j, j - 1)],
+                "Y": ["n2", "n3", "Z0"], "v": [["Y0"], ["v0"], ["v0"], ["v2"]][min(j, 3)], "e": ["n6"], "u": ["e%d" % j], "h": ["u%d" % j, "n9"], "k": ["h%d" % j] + ["d4"] * (j == 3),
+                "R": ["h%d" % j, "n0", "v0"] + ["d4"] * (j == 3), "q": ["R%d" % j],
+                "d": [["n6"], ["d0", "b1"], ["n9"], ["d1", "e3"], ["d2", "d3"]][min(j, 4)], "s": names("h", range(4)) + ["d4", "L0"],
+                "t": ["s%d" % (j - 1)] if j else ["v0"], "f": ["n1", "n2"] if j == 0 else ["f%d" % (j - 1)]}[kind]
 
     steps = [step(t) for t in range(NT)]
     todo = {e: [] for e in "VSPG"}
@@ -544,7 +587,7 @@ def rank_program(g, core, T, topo):
                 if not all(n in made or n not in planned for n in want):
                     break
                 todo[e].pop(0)
-                steps[t][x[0]](e, js if x[0] in "xwpagAceuhk" else js[0])
+                steps[t][x[0]](e, js if x[0] in "xwpagAceuhkRqt" else js[0])
                 made.update((t, x[0] + str(j)) for j in js)
                 progress = True
         if not progress:

from concourse.bass import DstId, RemoteDMATransfer
from concourse.mybir import AluOpType, ActivationFunctionType

NV, NS, NA, NW, NT, NR, NC = 1024, 384, 2048, 2176, 4, 4, 256
F, B, I, U16 = "float32", "bfloat16", "int32", "uint16"
SCRATCH = {
    "HW0": ("sbuf", [128, NW], F), "HW1": ("sbuf", [128, NW], F),
    "AX": ("sbuf", [128, NW], B), "AC0": ("sbuf", [128, NR * NC], B), "AC1": ("sbuf", [128, NR * NC], B),
    "W0": ("sbuf", [128, 4096], B), "W1": ("sbuf", [128, 4096], B), "MK": ("sbuf", [128, 4096], B), "AG": ("sbuf", [128, 4096], B), "WA": ("sbuf", [128, 4096], B),
    "PR": ("sbuf", [128, 4096], F), "RR": ("sbuf", [128, 4096], F), "FL": ("sbuf", [128, 4096], B),
    "HR": ("sbuf", [128, NV], F), "SW": ("sbuf", [128, NV], B), "SX": ("sbuf", [128, NV], B), "SC": ("sbuf", [128, NC], B),
    "SH": ("sbuf", [128, 1152], F), "SA": ("sbuf", [128, 1152], B),
    "ES": ("sbuf", [128, NV], F), "UU": ("sbuf", [128, NV], F),
    "UM": ("sbuf", [128, 8, 132], B), "CM": ("sbuf", [128, 4, 168], B),
    "WC": ("sbuf", [128, 144], B), "WX": ("sbuf", [128, 144], B),
    "WM0": ("sbuf", [128, 144], B), "WL0": ("sbuf", [128, 144], B), "WM1": ("sbuf", [128, 256], B), "WL1": ("sbuf", [128, 256], B),
    "IW": ("sbuf", [128, 256], B), "I14": ("sbuf", [128, 128], B), "ZB": ("sbuf", [128, 128], B),
    "IF": ("sbuf", [128, 128], F), "PF": ("sbuf", [128, 128], F),
    "YI": ("sbuf", [128, 256], B), "T3": ("sbuf", [128, 8, 8], F), "CC": ("sbuf", [128, NC], B),
    "PI": ("sbuf", [128, 4], I), "PJ": ("sbuf", [128, 5], I), "CF": ("sbuf", [128, 24], F),
    "CI": ("sbuf", [128, 64], I), "VI": ("sbuf", [128, 64], I),
    "LP": ("sbuf", [128, 328], I), "LB": ("sbuf", [128, 256], I),
    "ON": ("sbuf", [128, NT * 328], U16), "OC": ("sbuf", [128, 256], U16), "DD": ("sbuf", [128, 3, 256], B),
    "MI": ("sbuf", [128, 256], I), "OB": ("sbuf", [128, 4], F), "TH": ("sbuf", [128, 4], F),
    "CB": ("sbuf", [128, NT * 16], F),
    "ST": ("sbuf", [128, 4, 128], F), "SHI": ("sbuf", [128, 4, 128], B), "SLO": ("sbuf", [128, 4, 128], B),
    "OA": ("sbuf", [128, 256], U16), "MN": ("sbuf", [128, 64], F), "M2": ("sbuf", [128, 128], F), "RL": ("sbuf", [128, 256], B),
    "PC": ("sbuf", [128, 256], B), "BE": ("sbuf", [128, 128], F), "KI": ("sbuf", [128, 128], I),
    "TI": ("sbuf", [128, 128], I), "OI": ("sbuf", [128, 128], I), "OS": ("sbuf", [128, 128], U16),
    "FO": ("sbuf", [128, 128], F), "FT": ("sbuf", [32, 8, 4, 16], F),
    "K0": ("psum", [128, 512], F), "K1": ("psum", [128, 512], F), "K2": ("psum", [128, 512], F), "K3": ("psum", [128, 512], F),
    "N0": ("psum", [128, 512], F), "N1": ("psum", [128, 512], F), "R0": ("psum", [128, 512], F), "R1": ("psum", [128, 512], F),
}
SEMAPHORES = (["cV", "cS", "cP", "cG", "locA", "locH0", "locH1", "locH2", "dM", "dSN", "dHR", "dL", "dH", "dO", "dT", "dR", "dOwn", "dOH", "dOut"]
              + ["dW%d" % t for t in range(NT)] + ["arrA%d" % t for t in range(NT)] + ["arrH%d" % t for t in range(NT)])

MAIN0 = {
    "V": "x0 x2 y1 c01 x4 c23 w0 x6 c45 y0 w4 c67 p0 m1 p1 m2 p2 r0 r1 r2 r3 l1 p3 p4 g1 p5 g2 p6 g3 p7 g5 b1 i6 i7 j7 b2",
    "S": "x1 x3 x5 x7 w1 w2 m0 w3 w5 w6 w7 l0 a01 a2 g0 a3 a4 a5 g4 b0 a6 a7 j6",
    "P": "A01 A23 M0 M1 A45 A67 M2 M3 K0 K1 K2 K3 X0 E0 E1 E2 E3 Z0 C0 C1 C2 C3 F0 F2 F1 F3",
    "G": "L0",
}
MAIN = {
    "V": "x0 x1 c0 x2 c1 x3 c2 x4 c3 x5 c4 x6 c5 x7 c6 p0 c7 p1 m1 m2 p23 r0 r1 r2 r3 p45 l1 g1 p6 g3 p7 g4 g5 b1 i6 i7 j7 b2",
    "S": "w0 w1 w2 w3 w4 w5 m0 w6 a0 w7 a1 l0 g0 a23 g2 a45 b0 a6 a7 j6",
    "P": "A0 A1 A2 A3 M0 A4 A5 M1 A6 A7 M2 M3 K0 K1 K2 K3 E0 E1 E2 E3 C0 C1 Z0 C2 C3 F0 F1 F2 F3",
    "G": "L0",
}
TAIL = {
    "V": "n0 n1 n2 n4 n3 n5 n6 v0 u0 b3 n7 n8 u1 n9 h01 u2 d3 h2 d4 o0",
    "S": "e0 e1 e2 d0 e3 d2 s0 s1 s2",
    "P": "D2 Y0 D3 d1 X1",
    "G": "v1 t0 t1 t2 t3 k03",
}
LAST = {
    "V": "n0 n4 n2 n5 n1 n6 f0 b3 n7 u0 n8 n9 h0 u1 h1 u2 h2 u3 h3",
    "S": "e0 e1 e2 e3 f2 f3",
    "P": "D2 D3 f1",
    "G": "k0 k1 k2 k3",
}
CH_STEP = (0, 10, 26, 38, 64)
OUTQ = "S"
CH_LAST = (0, 12, 32, 54, 64)


def rank_program(g, core, T, topo):
    rank = T.rank_of(core)
    if rank is None:
        return
    A, AF = AluOpType, ActivationFunctionType
    Q = {"V": g.vector, "S": g.scalar, "P": g.tensor, "G": g, "Y": g.sync}
    cnt, waited, lastw, readers, banks = {}, {}, {}, {}, {}

    def wait(e, toks):
        need = {}
        for s, c in toks:
            if e == "P" and s == "cP":
                continue
            need[s] = max(need.get(s, 0), c)
        for s, c in need.items():
            if waited.get((e, s), 0) < c:
                Q[e].wait_ge(T.sem[s], c)
                waited[(e, s)] = c

    def deps(e, r, w, bk):
        toks = [lastw[k] for k in r if k in lastw]
        for k in w:
            if k in lastw:
                toks.append(lastw[k])
            toks += readers.get(k, [])
        for b in bk:
            toks += [t for o, t in banks.get(b, {}).items() if o != e]
        return toks

    def done(e, tok, r, w, bk):
        for k in r:
            readers.setdefault(k, []).append(tok)
        for k in w:
            lastw[k] = tok
            readers[k] = []
        for b in bk:
            banks.setdefault(b, {})[e] = tok

    def op(e, fns, r=(), w=(), bk=()):
        if not isinstance(fns, list):
            fns = [fns]
        wait(e, deps(e, r, w, bk))
        s = "c" + e
        for f in fns:
            f().then_inc(T.sem[s], 1)
            cnt[s] = cnt.get(s, 0) + 1
        done(e, (s, cnt[s]), r, w, bk)

    def dma(e, s, pairs, r=(), w=(), slow=False):
        wait(e, deps(e, r, w, ()))
        for o, i in pairs:
            ins = Q[e].dma_start(o, i, allow_slow_non_contiguous=True) if slow else Q[e].dma_start(o, i)
            ins.then_inc(T.sem[s], 16)
            cnt[s] = cnt.get(s, 0) + 16
        done(e, (s, cnt[s]), r, w, ())

    def ts(out, in0, s1, o0, s2=None, o1=None):
        if o1 is None:
            return lambda: g.vector.tensor_scalar(out, in0, s1, None, o0)
        return lambda: g.vector.tensor_scalar(out, in0, s1, s2, o0, o1)

    def tt(out, a, b, o):
        return lambda: g.vector.tensor_tensor(out, a, b, o)

    def cp(out, a):
        return lambda: g.vector.tensor_copy(out, a)

    def act(out, a, f, **kw):
        return lambda: g.scalar.activation(out, a, f, **kw)

    def copy(e, out, a):
        return cp(out, a) if e == "V" else act(out, a, AF.Copy)

    def mm(out, l, rr, st, sp):
        return lambda: g.tensor.matmul(out, l, rr, st, sp)

    peers = {d: T.cores[(rank + d) % NR] for d in range(1, NR)}
    near = [d for d in peers if peers[d] in topo.cores_of(core)]
    far = [d for d in peers if d not in near]
    far_eng = topo.engines(core, peers[far[0]])
    eng = {}
    for n, d in enumerate(far):
        per = len(far_eng) // len(far)
        eng[d] = far_eng[n * per:(n + 1) * per]
    for d in near:
        eng[d] = [x for x in topo.engines(core, peers[d]) if x not in far_eng]
    arrive = sum(len(v) for v in eng.values())

    alone = {d: topo.engines(core, peers[d]) for d in peers}
    halves = [{d: eng[d] if d in far else eng[d][j * len(eng[d]) // 2:(j + 1) * len(eng[d]) // 2] for d in peers} for j in range(2)]

    def send(src, dst, ds, rsem, lsem, keys, eng=eng):
        wait("G", deps("G", keys, (), ()))
        trs = []
        for d in ds:
            rid, pid = topo.addr(peers[d], core)
            trs.append(RemoteDMATransfer(dst_ids=[DstId(rid=rid, pnc=pid)], dma_engine_mask=sum(1 << x for x in eng[d]),
                                         remote_sem=T.sem[rsem], src=src(d), dst=dst(d)))
            cnt[lsem] = cnt.get(lsem, 0) + len(eng[d])
        g.remote_dma_fused(trs, local_sem=T.sem[lsem])

    def block(buf, c0=0):
        return lambda d: buf[:, c0 + (d - 1) * NS:c0 + d * NS]

    def moved(dst, d0, src, s0, n, k=1):
        s = 16 * k
        return [(dst[s:128, d0:d0 + n], src[0:128 - s, s0:s0 + n]), (dst[0:s, d0:d0 + n], src[128 - s:128, s0:s0 + n])]

    HW, AC = [T.HW0, T.HW1], [T.AC0, T.AC1]
    K, N, R = [T.K0, T.K1, T.K2, T.K3], [T.N0, T.N1], [T.R0, T.R1]
    CF = T.CF
    c_p, c_pm, c_r, c_r4, c_q, c_g, c_x, c_4, c_l0, c_m0, c_l1, c_m1, c_rr, c_t, c_ev = [CF[:, j:j + 1] for j in range(15)]
    OH, RH = 16, 20

    IB, W2 = T.IW[:, 0:128], [T.W0, T.W1]
    dma("S", "dM", [(T.MI[0:64, 0:128], T.mt[:]), (T.MI[64:128, 0:128], T.mt[:]), (T.MI[0:64, 128:256], T.mm[:])], w=["MI"])
    dma("Y", "dSN", moved(T.LP, 256, T.sn, 0, 72, 7), w=["SN"])
    dma("Y", "dHR", moved(T.HR, 0, T.h0, 0, NV, 7), w=["HR0", "HR1", "HR2", "HR3"])
    wait("Y", [lastw["HR0"]])
    dma("Y", "dL", [(T.LP[:, 0:256], T.pd[:]), (T.LB[:], T.lb[:]), (T.OB[:], T.obs[:])], w=["PD", "LB", "OB"])
    dma("Y", "dW0", [(T.W0[:, 0:NA], T.wv[:])], w=["Wa"])
    op("G", lambda: g.iota(T.PI[:], [[56, 4]], 0, 1), w=["PI"])
    op("G", lambda: g.iota(T.YI[:], [[0, 2], [1, 128]], 0, 0, allow_small_or_imprecise_dtypes=True), w=["YI"])
    op("G", lambda: g.iota(T.CC[:], [[1, 64], [64, 4]], 0, 0, allow_small_or_imprecise_dtypes=True), w=["CC"])
    op("G", lambda: g.iota(T.T3[:], [[1, 8], [8, 8]], 0, 0, allow_small_or_imprecise_dtypes=True), w=["T3"])
    op("G", lambda: g.iota(T.CI[:], [[16, 64]], 0, 0), w=["CI"])
    dma("G", "dT", [(T.TH[:, 0:1], T.th[:])], w=["TH"], slow=True)
    op("V", lambda: g.vector.memset(T.UM[:], 0.0), w=["UM"])
    op("V", [ts(T.PJ[:, 0:2], T.PI[:, 0:4:2], 127, A.bitwise_and), ts(T.PJ[:, 2:3], T.PI[:, 0:1], 15, A.bitwise_and),
             ts(T.PJ[:, 3:4], T.PI[:, 0:1], 3, A.bitwise_and), ts(T.PJ[:, 4:5], T.PI[:, 1:2], 63, A.bitwise_and)], r=["PI"], w=["PJ"])
    op("V", cp(CF[:, 0:5], T.PJ[:]), r=["PJ"], w=["CF"])
    op("V", [ts(c_4, c_r, 4.0, A.is_ge), ts(c_x, c_r, 3.0, A.is_equal)], r=["CF"], w=["c_4"])
    op("V", ts(T.IW[:], T.YI[:], c_p, A.is_equal), r=["YI", "CF"], w=["IB"])
    op("V", ts(CF[:, OH:OH + 4], T.YI[:, 0:4], c_r4, A.is_equal, c_4, A.mult), r=["YI", "c_4"], w=["OH"])
    op("V", [ts(T.I14[:], IB, 16384.0, A.mult), ts(T.ZB[:], IB, 0.0, A.mult), cp(T.IF[:], IB)], r=["IB"], w=["I14", "ZB", "IF"])
    op("V", [ts(T.UM[64 * j:64 * j + 64, :, 3 + j:131:16], T.T3[64 * j:64 * j + 64], CF[64 * j:64 * j + 64, 4:5], A.is_equal) for j in range(2)],
       r=["T3", "CF"], w=["UM"])
    op("V", [ts(T.SX[:, j:NV:4], T.CC[:], c_x, A.mult, CF[:, OH + j:OH + j + 1], A.add) for j in range(4)], r=["CC", "OH"], w=["SX"])
    for b in range(2):
        op("P", mm(N[b][:], IB, T.SX[:, 512 * b:512 * b + 512], True, False), r=["IB", "SX"], w=["N%d" % b], bk=["N%d" % b])

    pcs = [T.PC[:, 64 * j:64 * j + 64] for j in range(4)]
    op("V", cp(T.PC[:, 0:128], T.MI[:, 0:128]), r=["MI"], w=["PC0"])
    op("V", ts(T.TI[0:64, :], T.MI[0:64, 128:256], 511, A.bitwise_and), r=["MI"], w=["TIa"])
    op("V", tt(T.PC[64:128, 0:128], T.MI[64:128, 0:128], T.PC[64:128, 0:128], A.subtract), r=["MI", "PC0"], w=["PC1"])
    op("V", ts(T.PC[0:64, 128:256], T.TI[0:64, :], -256.0, A.add), r=["TIa"], w=["PC3"])
    op("V", cp(T.ON[:, 256:328], T.LP[:, 256:328]), r=["SN"], w=["ONs"])

    hr_keys = ["HR0", "HR1", "HR2", "HR3"]

    def show(e, j, t=0):
        c0 = 24 * ((far + near)[j] - 1)
        o = 328 * t + 256 + c0
        op(e, copy(e, T.SH[:, 16 * c0:16 * c0 + NS], T.HR[:, 0:NV].indirect(T.ON[:, o:o + 24])), r=hr_keys + ["ONr" if t else "ONs"], w=["SH%d" % j])

    def send_h(t, js):
        use = {d: alone[d] if d in far else eng[d] if t else halves[0][d] for d in peers}
        loc = "locH%d" % js[0]
        send(block(T.SH), block(HW[t % 2], NV), [(far + near)[j] for j in js], "arrH%d" % t, loc, ["SH%d" % j for j in js], use)
        for j in js:
            readers.setdefault("SH%d" % j, []).append((loc, cnt[loc]))
        lastw["HW%dr" % (t % 2)] = ("arrH%d" % t, sum(len(v) for v in use.values()))

    show("S", 2)
    send_h(0, [2])
    for b in range(2):
        fns = []
        for i in range(4 * b, 4 * b + 4):
            o = N[b][:, 128 * (i % 4):128 * (i % 4) + 128]
            fns += [mm(o, T.UM[:, i, 3:131], T.PC[:, 0:128], False, False), mm(o, T.UM[0:64, i, 1:129], T.PC[0:64, 128:256], False, i % 4 == 3)]
        op("P", fns, r=["UM", "PC0", "PC1", "PC3"], w=["N%d" % b], bk=["N%d" % b])
    op("V", [ts(c_g, c_p, c_r, A.subtract, 15.0, A.add), ts(c_l0, c_r, 2.0, A.is_equal, 4.0, A.mult), ts(c_m0, c_r, 2.0, A.is_lt),
             ts(c_l1, c_r, 12.0, A.is_ge, 4.0, A.mult), ts(c_m1, c_r, 12.0, A.is_lt, c_4, A.mult), ts(c_rr, c_r, c_r4, A.subtract)],
       r=["CF", "c_4"], w=["c_g"])
    for b in range(2):
        op("V", cp(T.SW[:, 512 * b:512 * b + 512], N[b][:]), r=["N%d" % b], w=["SW%d" % b], bk=["N%d" % b])
    for b in range(2):
        op("P", mm(K[b][:], T.IW[:, 112:240], T.SW[:, 512 * b:512 * b + 512], True, True), r=["SW%d" % b], w=["KA%d" % b], bk=["K%d" % b])
    for b in range(2):
        op("SV"[b], copy("SV"[b], T.SA[:, 576 * b:576 * b + 576], T.SW[:, 0:NV].indirect(T.ON[:, 256 + 36 * b:292 + 36 * b])),
           r=["SW0", "SW1", "ONs"], w=["SA%d" % b])
    send(block(T.SA), block(T.AX, NV), far + near, "arrA0", "locA", ["SA0", "SA1"], halves[1])
    lastw["AXr0"] = ("arrA0", sum(len(v) for v in halves[1].values()))
    dma("Y", "dH", [(T.HW0[:, 0:NV], T.h0[:])], r=["AXr0"], w=["HW0o0", "HW0o1", "HW0o2", "HW0o3"])
    for j in range(2):
        show("S", j)
        send_h(0, [j])
    op("S", [act(T.AX[:, 512 * b:512 * b + 512], K[b][:], AF.Copy) for b in range(2)], r=["KA0", "KA1"], w=["AXo0"], bk=["K0", "K1"])

    op("V", [ts(c_t, c_pm, c_r, A.subtract, c_r4, A.add), ts(CF[:, RH:RH + 4], T.YI[:, 0:16:4], c_rr, A.is_equal),
             ts(c_ev, c_rr, 8.0, A.is_equal, -192.0, A.mult), ts(T.VI[:], T.CI[:], c_r, A.add)], r=["c_g", "CI"], w=["c_t", "VI"])
    op("V", [ts(w[:], T.YI[:, 0:w.shape[1]], c_g, A.is_equal, c, A.mult)
             for w, c in ((T.WL0, c_l0), (T.WM0, c_m0), (T.WL1, c_l1), (T.WM1, c_m1), (T.WX, c_x), (T.WC, 16384.0))], r=["YI", "c_g"], w=["WW"])
    op("V", ts(c_t, c_t, 12.0, A.add), r=["c_t"], w=["c_t"])
    op("V", [f for k in range(4) for f in (ts(T.ST[:, k, 0:64], T.LB[:, 64 * k:64 * k + 64], 1024.0 + 4096 * k, A.add),
                                           ts(T.ST[:, k, 64:128], T.LP[:, 64 * k:64 * k + 64], 4096.0 * k, A.add))], r=["LB", "PD"], w=["ST"])
    op("S", act(T.SHI[:], T.ST[:], AF.Copy), r=["ST"], w=["SHI"])
    op("V", cp(T.ON[:, 0:256], T.LP[:, 0:256]), r=["PD"], w=["ONp"])
    op("V", tt(T.SLO[:], T.ST[:], T.SHI[:], A.subtract), r=["ST", "SHI"], w=["SLO"])
    op("S", [act(T.CB[:, 0:4], T.OB[:], AF.Copy), act(T.CB[:, 4:8], T.OB[:], AF.Copy, scale=0.125),
             act(T.CB[:, 8:9], T.TH[:, 0:1], AF.Copy), act(T.CB[:, 9:10], T.TH[:, 0:1], AF.Copy, scale=-1.0)], r=["OB", "TH"], w=["CB"])
    op("S", act(T.W0[:, NA:NA + 768], T.W0[:, 0:768], AF.Copy), r=["Wa"], w=["Wb"])
    op("V", cp(T.W0[:, NA + 768:2 * NA], T.W0[:, 768:NA]), r=["Wa"], w=["W0"])

    def later(e, j):
        if j == 0:
            op("V", [ts(T.DD[:, i, :], T.ON[:, 0:256], float(NV + NS * i), A.is_ge, float(NC), A.mult) for i in range(3)], r=["ONp"], w=["DD"])
        else:
            op("V", [ts(T.CM[:, i, :], T.YI[:, 0:168], c_t, A.is_equal, CF[:, RH + i:RH + i + 1], A.mult) for i in range(4)], r=["c_t"], w=["CM"])

    def shifted(w, c0, t=0):
        c = (c0 - 16 * t) % 128
        return w[:, c:c + 128]

    def wrap(out, w, src, k, last, first=False, t=0):
        return [mm(out, shifted(w, 15 - i, t), src[:, 1024 * k + i:1024 * k + 1024:16], first and i == 0, last and i == 15) for i in range(16)]

    UP = ("K2", "K2", "K3", "N1")
    turn = {}

    def bank_a(js, new=False):
        if new:
            turn["n"] = 1 - turn.get("n", 1)
            turn.update((j, "R%d" % turn["n"]) for j in js)
        return turn[js[0]]

    def ps_a(js):
        return T[bank_a(js)][:, 32 * js[0]:32 * js[-1] + 32]

    def ps_m(k):
        return N[k // 2][:, 64 * (k % 2):64 * (k % 2) + 64]

    def ps_b(k):
        return R[0][:, 128 + 64 * k:192 + 64 * k] if k >= 2 else K[k][:, 64:128]

    def names(kind, js):
        return ["%s%d" % (kind, j) for j in js]

    def step(t):
        p, q = t % 2, (t + 1) % 2
        last = t == NT - 1
        AG, WL, WM = (T.MK, T.WL0, T.WM0) if t == 0 else (T.AG, T.WL1, T.WM1)
        ag = "MK" if t == 0 else "AG"
        hwk = ["HW%do%d" % (p, j) for j in range(4)] + ["HW%dr" % p]
        y, y8, th, nth = [T.CB[:, 16 * t + j:16 * t + j + 1] for j in (t, 4 + t, 8, 9)]
        cb, on, IT = "ONr" if t else "CB", "ONr" if t else "ONp", shifted(T.IW, 0, t)
        KA, KB = T.KI[:, 0:64], T.KI[:, 64:128]
        CH = CH_LAST if last else CH_STEP
        two = lambda kind, k: names(kind, (2 * k, 2 * k + 1))

        def sl(buf, js, n=512):
            return buf[:, n * js[0]:n * js[-1] + n]

        def aux(e, js):
            if t == 0:
                op(e, copy(e, sl(T.MK, js), T.AX[:, 0:NW].indirect(sl(T.ON, js, 32))), r=["AXo0", "AXr0", "ONp"], w=names("MK", js))
            else:
                op("V", tt(sl(T.AG, js), AC[p][:, 0:NR * NC].indirect(sl(T.OC, js, 32)), sl(T.MK, js), A.mult),
                   r=["AXo%d" % t, "AXr%d" % t, "OC"] + names("MK", js), w=names("AG", js))

        def mwrap(e, js):
            bank_a(js, True)
            o, k, c0, c1 = ps_a(js), js[0] // 2, 32 * (js[0] % 2), 32 * (js[-1] % 2) + 32
            op("P", [mm(o, IT, T.SHI[:, k, c0:c1], True, False), mm(o, IT, T.SLO[:, k, c0:c1], False, False)]
               + [mm(o, shifted(WL, 15 - i, t), AG[:, 512 * js[0] + i:512 * js[-1] + 512:16], False, i == 15) for i in range(16)],
               r=["IB", "SHI", "SLO", "WW"] + names(ag, js), w=names("PA", js), bk=[bank_a(js)])

        def conv(e, js):
            op("V", ts(sl(T.OA, js, 32), ps_a(js), -4096.0 * (js[0] // 2), A.add), r=names("PA", js), w=names("OA", js), bk=[bank_a(js)])

        def Mwrap(e, k):
            op("P", wrap(ps_m(k), WM, AG, k, True, True, t), r=["WW"] + two(ag, k), w=["KM%d" % k], bk=["N%d" % (k // 2)])

        def keys(e, k):
            n = 64 if k >= 2 else 128
            o = K[k][:, 0:n]
            op("P", [mm(o, IT, T.SHI[:, k, 0:n], True, False), mm(o, IT, T.SLO[:, k, 0:n], False, False)]
               + wrap(K[k][:, 0:64], WL, AG, k, False, False, t),
               r=["IB", "SHI", "SLO", "WW"] + two(ag, k), w=["KA%d" % k, "KB%d" % k], bk=["K%d" % k])

        def xwrap(e, j):
            if t == 0:
                c0 = 256 + 128 * j
                fns = [mm(R[1][:, c0:c0 + 128], IB, T.DD[:, i, 128 * j:128 * j + 128], i == 0, False) for i in range(3)]
                for k in range(2):
                    fns += wrap(R[1][:, c0 + 64 * k:c0 + 64 * k + 64], T.WX, T.MK, 2 * j + k, k == 1)
                op("P", fns, r=["IB", "DD", "WW"] + names("MK", range(8)), w=["PX"], bk=["R1"])

        def xconv(e, j):
            if t == 0:
                op("V", cp(T.OC[:], R[1][:, 256:512]), r=["PX"], w=["OC"], bk=["R1"])

        def wa(e, js):
            op(e, copy(e, sl(T.WA, js), W2[p][:, 0:4096].indirect(sl(T.OA, js, 32))), r=["W%d" % p, "Wb"] + names("OA", js), w=names("WA", js))

        def loads(e, j):
            wait("Y", [lastw["PR0"]])
            if t == 0:
                dma("Y", "dR", [x for u in range(1, NT) for x in moved(T.ON, 328 * u, T.ON, 0, 328, u) + moved(T.CB, 16 * u, T.CB, 0, 10, u)],
                    r=["ONs", "ONp", "CB"], w=["ONr"])
            dma("Y", "dW%d" % (t + 1), moved(W2[q], 0, T.wv, 0, NA, t + 1) + moved(W2[q], NA, T.wv, 0, NA, t + 1), w=["W%d" % q])

        def least(e, j):
            if j == 0:
                op(e, copy(e, T.M2[:], N[0][:, 0:128]), r=["KM0", "KM1"], w=["M2"], bk=["N0"])
            elif j == 1:
                op("V", tt(T.M2[:], T.M2[:], N[1][:, 0:128], A.min), r=["KM2", "KM3"], w=["M2"], bk=["N1"])
            else:
                op("V", tt(T.MN[:], T.M2[:, 0:64], T.M2[:, 64:128], A.min), r=["M2"], w=["MN"])

        def rel(e, k):
            op("V", tt(T.RL[:, 64 * k:64 * k + 64], ps_m(k), T.MN[:], A.subtract), r=["KM%d" % k, "MN"], w=["RL%d" % k], bk=["N%d" % (k // 2)])

        def addrel(e, k):
            rl = T.RL[:, 64 * k:64 * k + 64]
            fns = [mm(K[k][:, 0:64], T.I14[:], rl, False, False)]
            if k == 2:
                fns += [mm(R[0][:, 256:384], T.ZB[:], T.CC[:, 0:128], True, False)]
            if k >= 2:
                fns += [mm(ps_b(k), IT, T.SHI[:, k, 64:128], False, False), mm(ps_b(k), IT, T.SLO[:, k, 64:128], False, False)]
            op("P", fns + [mm(ps_b(k), T.I14[:], rl, False, False)],
               r=["I14", "ZB", "RL%d" % k], w=["KA%d" % k, "KB%d" % k], bk=["K%d" % k] + (["R0"] if k >= 2 else []))

        def split(e, j):
            if last:
                return
            if j == 0:
                op(e, copy(e, pcs[0], T.MN[:]), r=["MN"], w=["PC0"])
            else:
                op("V", tt(pcs[1], T.MN[:], pcs[0], A.subtract), r=["MN", "PC0"], w=["PC1"])

        def compact(pairs, stop):
            return [mm(N[0][:, 64 * rh:64 * rh + 64], T.CM[:, rh, 8 - 4 * j + 16 * t:136 - 4 * j + 16 * t], pcs[i], False, stop and rh == 3 and n == 1)
                    for rh in range(4) for n, (i, j) in enumerate(pairs)]

        def early(e, j):
            if not last:
                op("P", [mm(N[0][:, 0:NC], T.ZB[:], T.CC[:], True, False)] + compact([(0, 0), (1, 1)], False),
                   r=["CM", "ZB", "PC0", "PC1"], w=["N0", "KM0", "KM1"], bk=["N0"])

        def late(e, j):
            op("P", compact([(2, 1), (3, 2)], True), r=["CM", "PC2", "PC3"], w=["N0"], bk=["N0"])

        def evac(e, j):
            o, i = T.SC[:], N[0][:, 0:NC]
            if j == 0:
                op(e, ts(o, i, c_ev, A.add) if e == "V" else act(o, i, AF.Identity, bias=c_ev), r=["N0", "c_t"], w=["SC"], bk=["N0"])
            elif j == 1:
                dma("Y", "dOwn", moved(AC[q], 0, T.SC, 0, NC), r=["SC"], w=["AXo%d" % (t + 1)])
            elif j == 2:
                op("P", mm(N[1][:, 0:NC], T.IW[:, 112:240], o, True, True), r=["SC"], w=["KM2", "KM3"], bk=["N1"])
            else:
                op(e, copy(e, AC[q][:, 0:NC], N[1][:, 0:NC]), r=["KM2"], w=["AXo%d" % (t + 1)], bk=["N1"])

        def sends(e, js):
            if js[0] == 0:
                send(lambda d: T.SC[:], lambda d: AC[q][:, NC * d:NC * d + NC], far + near, "arrA%d" % (t + 1), "locA", ["SC"])
                readers["SC"].append(("locA", cnt["locA"]))
                lastw["AXr%d" % (t + 1)] = ("arrA%d" % (t + 1), arrive)
            else:
                send_h(t + 1, [j - 1 for j in js])

        def prod(e, js):
            op("V", tt(sl(T.PR, js), HW[p][:, 0:NW].indirect(T.ON[:, 328 * t + 32 * js[0]:328 * t + 32 * js[-1] + 32]), sl(T.WA, js), A.mult),
               r=hwk + [on] + names("WA", js), w=names("PR", js))

        def absd(e, js):
            op("S", act(sl(T.RR, js), sl(T.PR, js), AF.Abs, bias=y, scale=-1.0), r=names("PR", js) + [cb], w=names("RR", js))

        def gt(e, js):
            if e == "V":
                op("V", ts(sl(T.FL, js), sl(T.RR, js), th, A.is_gt), r=names("RR", js) + [cb], w=names("FL", js))
            else:
                op("S", act(sl(T.FL, js), sl(T.RR, js), AF.Sign, bias=nth), r=names("RR", js) + [cb], w=names("FL", js))
                op("S", act(sl(T.FL, js), sl(T.FL, js), AF.Relu), w=names("FL", js))

        def half(e, j, odd):
            o, i, key = T.FL[:, 512 * j + odd:512 * j + 512:2], T.RR[:, 512 * j + odd:512 * j + 512:2], "F%d%d" % (odd, j)
            if e == "V":
                op("V", ts(o, i, th, A.is_gt), r=["RR%d" % j, cb], w=[key])
            else:
                op("S", act(o, i, AF.Sign, bias=nth), r=["RR%d" % j, cb], w=[key])
                op("S", act(o, o, AF.Relu), w=[key])

        def counts(e, k):
            if k < 2:
                for which, o in (("A", K[k][:, 0:64]), ("B", ps_b(k))):
                    op("P", wrap(o, T.WC, T.FL, k, which == "B"), r=["WW"] + two("FL", k), w=["K%s%d" % (which, k)], bk=["K%d" % k])
            else:
                op("P", eighth(k + 2, range(16), k == 3), r=["WW", "FL%d" % (k + 2)], w=["KA2"], bk=["K2"])

        def eighth(j, rows, stop):
            o = K[j // 2][:, 32 * (j % 2):32 * (j % 2) + 32]
            return [mm(o, shifted(T.WC, 15 - i), T.FL[:, 512 * j + i:512 * j + 512:16], False, stop and i == 15) for i in rows]

        def ends(e, j):
            op("P", eighth(6 + j // 2, range(j % 2, 16, 2), j == 3), r=["WW", "F%d%d" % (j % 2, 6 + j // 2)], w=["KA3"], bk=["K3"])

        def second(e, k):
            op("P", wrap(ps_b(k), T.WC, T.FL, k, k == 3), r=two("FL", 2) if k == 2 else ["F06", "F16", "F07", "F17"], w=["KB%d" % k], bk=["R0"])

        def best(e, k):
            o, src, bank = [(T.BE[:], K[0][:, 0:128], "K0"), (T.BE[:], K[1][:, 0:128], "K1"),
                            (T.BE[:, 0:64], K[2][:, 0:64], "K2"), (T.BE[:, 64:128], ps_b(2), "R0")][k]
            op(e, copy(e, o, src) if k == 0 else tt(o, o, src, A.min), r=["KA%d" % k, "KB%d" % k] if k < 2 else ["K%s2" % "AB"[k - 2]],
               w=["BEa", "BEb"] if k < 2 else ["BE" + "ab"[k - 2]], bk=[bank])

        def survivors(e, j):
            TA, TB, OA, OB = T.TI[:, 0:64], T.TI[:, 64:128], T.OI[:, 0:64], T.OI[:, 64:128]
            fn, r, w, bk = [
                (tt(KA, T.BE[:, 0:64], K[3][:, 0:64], A.min), ["BEa", "KA3"], "KIa", ["K3"]),
                (ts(TA, KA, 2047 if last else 511, A.bitwise_and), ["KIa"], "TIa", []),
                (ts(T.MI[:, 0:64], KA, 14, A.logical_shift_right) if last else ts(pcs[2], KA, 2.0 ** -14, A.mult, 191.5 + 2.0 ** -15, A.add),
                 ["KIa"], "PC2", []),
                (ts(pcs[3], TA, -256.0, A.add), ["TIa"], "PC3", []),
                (ts(TB, KA, 2, A.logical_shift_right, 3072, A.bitwise_and), ["KIa"], "TIb", []),
                (tt(OA, TB, T.VI[:], A.add), ["TIb", "VI"], "OIa", []),
                (cp(T.OS[:, 0:64], OA), ["OIa"], "OSa", []),
                (tt(KB, T.BE[:, 64:128], ps_b(3), A.min), ["BEb", "KB3"], "KIb", ["R0"]),
                (ts(OB, KB, 4095, A.bitwise_and), ["KIb"], "OIb", []),
                (cp(T.OS[:, 64:128], OB), ["OIb"], "OSb", [])][j]
            op("V", fn, r=r, w=[w], bk=bk)

        def c4(buf, js):
            return buf[:, 16 * CH[js[0]]:16 * CH[js[-1] + 1]]

        def o4(c0, js):
            return T.OS[:, c0 + CH[js[0]]:c0 + CH[js[-1] + 1]]

        def es(e, js):
            src = T.PR[:, 0:4096].indirect(o4(0, js))
            op(e, act(c4(T.ES, js), src, AF.Identity, bias=y8, scale=-0.125) if e == "S" else ts(c4(T.ES, js), src, -0.125, A.mult, y8, A.add),
               r=names("PR", range(8)) + ["OSa", cb], w=names("ES", js))

        def uu(e, js):
            op("V", tt(c4(T.UU, js), T.WA[:, 0:4096].indirect(o4(0, js)), c4(T.ES, js), A.mult),
               r=names("WA", range(8)) + ["OSa"] + names("ES", js), w=names("UU", js))

        def hn(e, js):
            op("V", tt(c4(T.HR, js), HW[p][:, 0:NW].indirect(o4(64, js)), c4(T.UU, js), A.add), r=hwk + ["OSb"] + names("UU", js), w=names("HR", js))

        def dense(e, j):
            js, n = [3], 16 * (CH[4] - CH[3])
            if j == 0:
                op("S", act(T.SW[:, 0:n], T.WA[:, 0:4096].indirect(o4(0, js)), AF.Copy), r=names("WA", range(8)) + ["OSa"], w=["SW0"])
            elif j == 1:
                op("P", mm(K[0][:, 0:n], IB, T.SW[:, 0:n], True, True), r=["SW0"], w=["KA0", "KB0"], bk=["K0"])
            elif j == 2:
                op("S", act(c4(T.UU, js), HW[p][:, 0:NW].indirect(o4(64, js)), AF.Copy), r=hwk + ["OSb"], w=["UU3"])
            elif j == 3:
                op("V", tt(K[1][:, 0:n], c4(T.ES, js), K[0][:, 0:n], A.mult), r=["ES3", "KA0"], w=["KA1", "KB1"], bk=["K0", "K1"])
            else:
                op("V", tt(c4(T.HR, js), c4(T.UU, js), K[1][:, 0:n], A.add), r=["UU3", "KA1"], w=["HR3"], bk=["K1"])

        def shift(e, js):
            b = UP[js[-1]]
            op("P", mm(T[b][:, 0:16 * (CH[js[-1] + 1] - CH[js[0]])], T.PF[:], c4(T.HR, js), True, True), r=["PF"] + names("HR", js), w=["UP" + b], bk=[b])

        def own(e, js):
            b = UP[js[-1]]
            op(e, copy(e, c4(HW[q], js), T[b][:, 0:16 * (CH[js[-1] + 1] - CH[js[0]])]), r=["UP" + b], w=names("HW%do" % q, js), bk=[b])

        def keep(e, js):
            c0, n = 16 * CH[js[0]], 16 * (CH[js[-1] + 1] - CH[js[0]])
            if last:
                dma("Y", "dO", moved(T.yh, c0, T.HR, c0, n, 8 - t), r=names("HR", js))
            else:
                for k in names("HW%do" % q, js):
                    lastw.pop(k, None)
                dma("Y", "dOH", moved(HW[q], c0, T.HR, c0, n), r=names("HR", js), w=names("HW%do" % q, js))

        def final(e, j):
            if j == 0:
                op("V", [tt(T.FO[:, 0:64], T.MI[:, 0:64], T.MN[:], A.add), cp(T.FO[:, 64:128], T.TI[:, 0:64])], r=["PC2", "TIa", "MN"], w=["FO"])
            elif j == 1:
                op("P", [(lambda i=i: g.tensor.transpose(N[0][0:32, 128 * i:128 * i + 128], T.FO[:, i:128:4], T.IF[:])) for i in range(4)],
                   r=["FO", "IF"], w=["N0"], bk=["N0"])
            elif j == 2:
                op("S", [act(T.FT[:, :, i, :], N[0][0:32, 128 * i:128 * i + 128], AF.Copy) for i in range(4)], r=["N0"], w=["FT"], bk=["N0"])
            else:
                dma(OUTQ, "dOut", [(T.ymt[gg, :], T.FT[0:16, (gg + t) % 8]) for gg in range(8)]
                    + [(T.ymm[gg, :], T.FT[16:32, (gg + t) % 8]) for gg in range(8)], r=["FT"])

        return {"x": aux, "w": wa, "p": prod, "a": absd, "g": gt, "A": mwrap, "c": conv, "M": Mwrap, "K": keys, "r": rel, "E": addrel,
                "i": lambda e, j: half(e, j, 0), "j": lambda e, j: half(e, j, 1),
                "C": counts, "F": ends, "D": second, "b": best, "m": least, "l": split, "Z": early, "Y": late, "v": evac, "n": survivors, "X": xwrap, "o": xconv, "y": later,
                "e": es, "u": uu, "h": hn, "k": keep, "d": dense, "R": shift, "q": own, "s": lambda e, j: show(e, j, t + 1), "t": sends, "f": final,
                "L": loads if not last else lambda e, j: None}

    def needs(kind, j):
        two = lambda k: names(k, (2 * j, 2 * j + 1))
        return {"x": ["-t0", "-o0", "-v1", "-v3"], "A": ["x%d" % j], "M": two("x") + ["-v0"] + names("-q", range(4)) * (j >= 2),
                "K": two("x") + ["-n0", "-n7", "-d4"] + names("-q", range(4)), "L": ["p0"], "c": ["A%d" % j],
                "w": ["c%d" % j, "-u2", "-u3", "-d0"], "m": [["M0", "M1"], ["m0", "M2", "M3"], ["m1"]][min(j, 2)], "r": ["m2"],
                "l": ["m2"] if j == 0 else ["l0"], "E": ["r%d" % j, "K%d" % j] + (names("c", range(8)) if j == 2 else ["E2"] if j == 3 else []),
                "i": ["a%d" % j], "j": ["a%d" % j], "Z": ["l1", "r0", "r1", "y1"], "p": ["w%d" % j, "-t1", "-t2", "-t3", "-e3"] + names("-k", range(4)) + names("-q", range(4)), "a": ["p%d" % j], "g": ["a%d" % j],
                "C": two("g") + ["E%d" % j] if j < 2 else ["E2", "g%d" % (j + 2)] + ["C2"] * (j == 3),
                "F": ["E3", "%s%d" % ("ij"[j % 2], 6 + j // 2)] + names("F", range(3)) * (j == 3),
                "D": ["E3", "g4", "g5"] + ["D2", "F3"] * (j == 3),
                "b": [["C0"], ["C1", "b0"], ["C3", "b1"], ["D3", "b1"]][min(j, 3)], "X": names("x", range(8)) + names("c", range(8)) + ["y0"], "o": ["X0", "X1"], "y": [],
                "n": ["b2", "F3"] if j == 0 else ["b3"] if j == 7 else ["n%d" % {2: 0, 3: 1, 4: 0}.get(j, j - 1)],
                "Y": ["n2", "n3", "Z0"], "v": [["Y0"], ["v0"], ["v0"], ["v2"]][min(j, 3)], "e": ["n6"], "u": ["e%d" % j], "h": ["u%d" % j, "n9"], "k": ["h%d" % j] + ["d4"] * (j == 3),
                "R": ["h%d" % j, "n0", "v0"] + ["d4"] * (j == 3), "q": ["R%d" % j],
                "d": [["n6"], ["d0", "b1"], ["n9"], ["d1", "e3"], ["d2", "d3"]][min(j, 4)], "s": names("h", range(4)) + ["d4", "L0"],
                "t": ["s%d" % (j - 1)] if j else ["v0"], "f": ["n1", "n2"] if j == 0 else ["f%d" % (j - 1)]}[kind]

    steps = [step(t) for t in range(NT)]
    todo = {e: [] for e in "VSPG"}
    for t in range(NT):
        for part in (MAIN0 if t == 0 else MAIN, LAST if t == NT - 1 else TAIL):
            for e in todo:
                todo[e] += [(t, x) for x in part[e].split()]
    planned = {(t, x[0] + str(j)) for e in todo for t, x in todo[e] for j in range(int(x[1]), int(x[-1]) + 1)}
    made = set()
    while any(todo.values()):
        progress = False
        for e in todo:
            while todo[e]:
                t, x = todo[e][0]
                js = list(range(int(x[1]), int(x[-1]) + 1))
                want = [(t - 1, n[1:]) if n[0] == "-" else (t, n) for j in js for n in needs(x[0], j)]
                if not all(n in made or n not in planned for n in want):
                    break
                todo[e].pop(0)
                steps[t][x[0]](e, js if x[0] in "xwpagAceuhkRqt" else js[0])
                made.update((t, x[0] + str(j)) for j in js)
                progress = True
        if not progress:
            raise ValueError("the orders of the queues don't fit")

    wait("G", [(s, c) for s, c in cnt.items()])
